import numpy as np
import ml_dtypes


def mxq(x, axis, fmt="e4m3"):
    dtype, down = {"e4m3": (ml_dtypes.float8_e4m3fn, 7), "e5m2": (ml_dtypes.float8_e5m2, 14)}[fmt]
    v = np.moveaxis(np.asarray(x, np.float32).astype(ml_dtypes.bfloat16).astype(np.float64), axis, -1)
    blocks = v.reshape(v.shape[:-1] + (-1, 32))
    amax = np.abs(blocks).max(-1, keepdims=True)
    byte = np.maximum(np.where(amax > 0, np.frexp(amax)[1] - 1 + 127, 0) - down, 1)
    scale = np.exp2(byte - 127.0)
    codes = (blocks / scale).astype(np.float32).astype(dtype).astype(np.float64)
    return np.moveaxis((codes * scale).reshape(v.shape), -1, axis)


WIDE = False


def mx_kscale(k):
    if not WIDE:
        return np.ones(k)
    levels = np.array([10, -10, 5, -5, 0])
    if k % 512:
        return np.exp2(np.random.permutation(np.resize(levels, k // 32))).repeat(32)
    a = np.empty((k // 512, 16))
    for p in range(k // 512):
        a[p, :8] = np.random.permutation(np.resize(levels, 8))
        for g in range(8):
            far = levels[np.abs(levels - a[p, g]) >= 10]
            a[p, g + 8] = far[np.random.randint(len(far))]
    return np.exp2(a.ravel()).repeat(32)


def f64(x):
    return np.asarray(x).astype(np.float64)


def striped(idx):
    return np.tile(idx.reshape(-1, 16).T, (8, 1)).astype(np.uint16)


def unstriped(offs):
    return offs[:16].T.reshape(-1).astype(np.int64)


def striped8(idx):
    return np.concatenate([x.reshape(-1, 16).T for x in idx]).astype(np.uint16)


def runs(offs, k):
    lists = np.stack([offs[16 * r : 16 * r + 16].T.reshape(-1) for r in range(8)]).astype(np.int64)
    return lists[np.arange(k) % 512 // 64]


def pack_weight(w):
    k, n = w.shape
    w = f64(np.asarray(w, np.float32).astype(ml_dtypes.bfloat16)).reshape(k // 32, 32, n)
    amax = np.abs(w).max(1)
    byte = np.clip(np.where(amax > 0, np.frexp(amax)[1] - 1 + 127 - 7, 1), 1, 254)
    scaled = (w * np.exp2(127.0 - byte)[:, None, :]).reshape(k, n).astype(np.float32)
    words = np.ascontiguousarray(scaled.reshape(k // 512, 128, 4, n).transpose(0, 1, 3, 2)).astype(ml_dtypes.float8_e4m3fn).view(np.uint8)
    return words, np.ascontiguousarray(byte.astype(np.uint8).reshape(k // 512, 16, n))


def unpack_weight(words, scales):
    g, p, n, _ = words.shape
    vals = np.ascontiguousarray(words).view(ml_dtypes.float8_e4m3fn).astype(np.float64) * np.repeat(np.exp2(scales.astype(np.float64) - 127.0), 8, axis=1)[..., None]
    return vals.transpose(0, 1, 3, 2).reshape(g * 512, n)


E2M1 = np.array([0.0, 0.5, 1.0, 1.5, 2.0, 3.0, 4.0, 6.0, -0.0, -0.5, -1.0, -1.5, -2.0, -3.0, -4.0, -6.0])


def pack_fp4(w):
    k, n = w.shape
    w = f64(np.asarray(w, np.float32).astype(ml_dtypes.bfloat16)).reshape(k // 32, 32, n)
    amax = np.abs(w).max(1)
    mant, ex = np.frexp(amax / 6.0)
    byte = np.clip(np.where(amax > 0, np.where(mant > 0.5, ex, ex - 1) + 127, 1), 1, 254)
    scaled = (w * np.exp2(127.0 - byte)[:, None, :]).reshape(k, n).astype(np.float32)
    c = np.ascontiguousarray(scaled.reshape(k // 512, 128, 4, n).transpose(0, 1, 3, 2)).astype(ml_dtypes.float4_e2m1fn).view(np.uint8) & 0xF
    words = (c[..., 0::2] | (c[..., 1::2] << 4)).reshape(k // 512, 128, 2 * n)
    return np.ascontiguousarray(words), np.ascontiguousarray(byte.astype(np.uint8).reshape(k // 512, 16, n))


def unpack_fp4(words, scales):
    g, _, n = scales.shape
    words = np.ascontiguousarray(words).reshape(g, 128, n, 2)
    nib = np.empty((g, 128, n, 4), np.uint8)
    nib[..., 0::2] = words & 0xF
    nib[..., 1::2] = words >> 4
    vals = E2M1[nib] * np.repeat(np.exp2(scales.astype(np.float64) - 127.0), 8, axis=1)[..., None]
    return vals.transpose(0, 1, 3, 2).reshape(g * 512, n)


def relu(v):
    return np.maximum(v, 0.0)

def planes(y):
    n, m = y.shape
    v = y.astype(np.float32).astype(ml_dtypes.bfloat16).astype(np.float64).reshape(n // 32, 32, m)
    top = np.abs(v).max(1)
    byte = np.clip(np.where(top > 0, np.frexp(top)[1] - 1 + 127 - 7, 1), 1, 254)
    codes = (v * np.exp2(127.0 - byte)[:, None, :]).reshape(n, m).astype(np.float32).astype(ml_dtypes.float8_e4m3fn).view(np.uint8)
    words = codes.reshape(n // 512, 128, 4, m).transpose(0, 1, 3, 2)
    return np.ascontiguousarray(words), np.ascontiguousarray(byte.astype(np.uint8).reshape(n // 512, 16, m))


K, T, S, N, G, H = 512, 2048, 512, 512, 2048, 512
P = 2 ** 7


def setup_inputs():
    n = np.random.standard_normal
    s = mx_kscale(K)[:, None]
    u = mx_kscale(H)
    packed_xT = pack_weight(n((K, T)) * s)
    packed_dT = pack_weight(n((K, G)) / s)
    packed_w1 = pack_fp4(n((H, N)) / np.sqrt(H) / u[:, None])
    return {
        "x_words": packed_xT[0],
        "x_scales": packed_xT[1],
        "d_words": packed_dT[0],
        "d_scales": packed_dT[1],
        "cnt": np.tile(np.random.uniform(0.5, 1.5, S), (P, 1)).astype(np.float32),
        "gn": (np.random.uniform(0.5, 1.5, (H, 1)) * u[:, None]).astype(np.float32),
        "w1_words": packed_w1[0],
        "w1_scales": packed_w1[1],
        "offs": striped(np.random.permutation(T)[:S]),
        "kidx": striped8(np.random.randint(0, G, (8, H))),
    }


def reference(x_words, x_scales, d_words, d_scales, cnt, gn, w1_words, w1_scales, offs, kidx):
    d_kidx = unpack_weight(d_words, d_scales)[np.arange(K)[:, None], runs(kidx, K)]
    xq = unpack_weight(x_words, x_scales)[:, unstriped(offs)]
    s = 0.0625 * (d_kidx.T @ xq)
    rp = relu(s)
    z = f64(gn) * ((rp) ** 2)
    out_0 = ((unpack_fp4(w1_words, w1_scales).T @ mxq(z, 0, "e4m3"))) * f64(cnt)[:1]
    return (out_0,) + planes(out_0)

@@ -1,0 +1,157 @@
+from contextlib import ExitStack
+
+import concourse.mybir as mybir
+
+F32 = mybir.dt.float32
+BF16 = mybir.dt.bfloat16
+I32 = mybir.dt.int32
+U32 = mybir.dt.uint32
+U16 = mybir.dt.uint16
+U8 = mybir.dt.uint8
+FP8X4 = mybir.dt.float8_e4m3fn_x4
+FP4X4 = mybir.dt.float4_e2m1fn_x4
+ACT = mybir.ActivationFunctionType
+MULT = mybir.AluOpType.mult
+
+P = 128
+PACK = 4
+TABLE = 2048
+ENTRIES = 512
+CHUNK = 128
+CHUNKS = ENTRIES // CHUNK
+HALF = 256
+FLOPS = 2 * 2 * 512 * 512 * 512
+
+
+def tile_picked_reluattn_relu_po_kernel(tc, x_words, x_scales, d_words, d_scales, cnt, gn, w1_words, w1_scales, offs, kidx, out_0, out_1, out_2):
+    nc = tc.nc
+    with ExitStack() as ctx:
+        lists = ctx.enter_context(tc.tile_pool(name="lists", bufs=1))
+        keep = ctx.enter_context(tc.tile_pool(name="keep", bufs=1))
+        reuse = ctx.enter_context(tc.tile_pool(name="reuse", bufs=1))
+        psum = ctx.enter_context(tc.psum_pool(name="psum", bufs=1))
+
+        key_list = lists.tile([P, ENTRIES // 16], U16, name="key_list")
+        query_list = lists.tile([P, ENTRIES // 16], U16, name="query_list")
+        nc.sync.dma_start(key_list[:], kidx)
+        nc.sync.dma_start(query_list[:], offs)
+        gain_raw = keep.tile([P, PACK], F32, name="gain_raw")
+        nc.sync.dma_start(gain_raw[:], gn.rearrange("(p t) o -> p (t o)", t=PACK))
+
+        d_word_table = keep.tile([P, TABLE], I32, name="d_word_table", align_bytes=64)
+        x_word_table = keep.tile([P, TABLE], I32, name="x_word_table", align_bytes=64)
+        nc.sync.dma_start(d_word_table[:], d_words[0].rearrange("p n t -> p (n t)").bitcast(I32))
+        nc.sync.dma_start(x_word_table[:], x_words[0].rearrange("p n t -> p (n t)").bitcast(I32))
+
+        d_scale_table = reuse.tile([P, TABLE], U8, name="d_scale_table", align_bytes=64, offset=0)
+        x_scale_table = keep.tile([P, TABLE], U8, name="x_scale_table", align_bytes=64)
+        w_scale_raw = keep.tile([P, ENTRIES], U8, name="w_scale_raw", align_bytes=64)
+        nc.gpsimd.memset(d_scale_table[:].bitcast(I32), 0)
+        nc.vector.memset(x_scale_table[:].bitcast(I32), 0)
+        nc.gpsimd.memset(w_scale_raw[:].bitcast(I32), 0)
+        for v in range(2):
+            nc.scalar.dma_start(d_scale_table[v:P:16, :].bitcast(I32), d_scales[0][v:16:2, :].bitcast(I32))
+        for q in range(4):
+            nc.scalar.dma_start(x_scale_table[32 * q : 32 * q + 4, :].bitcast(I32), x_scales[0][4 * q : 4 * q + 4, :].bitcast(I32))
+        for q in range(4):
+            nc.gpsimd.dma_start(w_scale_raw[32 * q : 32 * q + 4, :].bitcast(I32), w1_scales[0][4 * q : 4 * q + 4, :].bitcast(I32))
+
+        gain = keep.tile([P, PACK], F32, name="gain")
+        nc.scalar.activation(gain[:], gain_raw[:], ACT.Copy, scale=0.0625 * 0.0625)
+
+        d_scale_picked = reuse.tile([P, ENTRIES], U8, name="d_scale_picked", align_bytes=64, offset=4096)
+        d_scale = keep.tile([P, ENTRIES], U8, name="d_scale", align_bytes=64)
+        nc.vector.tensor_copy(d_scale_picked[:], d_scale_table[:].indirect(key_list[:]))
+        nc.vector.tensor_copy(d_scale[:].rearrange("p (t m) -> p t m", t=PACK), d_scale_picked[:].rearrange("p (m t) -> p t m", t=PACK))
+
+        w_word_raw = reuse.tile([P, 2 * ENTRIES], U8, name="w_word_raw", align_bytes=64, offset=0)
+        factor = reuse.tile([P, ENTRIES], F32, name="factor", align_bytes=64, offset=1024)
+        nc.sync.dma_start(w_word_raw[:].bitcast(I32), w1_words[0].bitcast(I32))
+        nc.sync.dma_start(factor[:], cnt)
+
+        for v in range(2):
+            nc.scalar.dma_start(d_scale[2 + v : P : 32, :].bitcast(I32), d_scale[16 + v : P : 32, :].bitcast(I32))
+
+        d_word_picked = reuse.tile([P, ENTRIES], U32, name="d_word_picked", align_bytes=64, offset=4096)
+        d_word = keep.tile([P, ENTRIES], U32, name="d_word", align_bytes=64)
+        nc.vector.tensor_copy(d_word_picked[:], d_word_table[:].bitcast(U32).indirect(key_list[:]))
+        nc.vector.tensor_copy(d_word[:].rearrange("p (t m) -> p m t", t=PACK), d_word_picked[:].rearrange("p (m t) -> p m t", t=PACK))
+
+        x_word = [keep.tile([P, HALF], U32, name="x_word%d" % h, align_bytes=64) for h in range(2)]
+        x_scale = [keep.tile([P, HALF], U8, name="x_scale%d" % h, align_bytes=64) for h in range(2)]
+
+        def gather_queries(h):
+            piece = query_list[:, h * HALF // 16 : (h + 1) * HALF // 16]
+            nc.vector.tensor_copy(x_scale[h][:], x_scale_table[:].indirect(piece))
+            nc.vector.tensor_copy(x_word[h][:], x_word_table[:].bitcast(U32).indirect(piece))
+
+        w_word = keep.tile([P, 2 * ENTRIES], U8, name="w_word", align_bytes=64)
+        w_scale = keep.tile([P, ENTRIES], U8, name="w_scale", align_bytes=64)
+
+        def deal_weights():
+            nc.vector.tensor_copy(w_word[:].rearrange("p (t m b) -> p t m b", t=PACK, b=2), w_word_raw[:].rearrange("p (m t b) -> p t m b", t=PACK, b=2))
+            nc.vector.tensor_copy(w_scale[:].rearrange("p (t m) -> p t m", t=PACK), w_scale_raw[:].rearrange("p (m t) -> p t m", t=PACK))
+
+        z_word = [keep.tile([P, CHUNK], U32, name="z_word%d" % c, align_bytes=64) for c in range(CHUNKS)]
+        z_scale = [keep.tile([P, CHUNK], U8, name="z_scale%d" % c, align_bytes=64) for c in range(CHUNKS)]
+        y_word = keep.tile([P, ENTRIES], U32, name="y_word", align_bytes=64)
+        y_scale = keep.tile([P, ENTRIES], U8, name="y_scale", align_bytes=64)
+        out_rows = out_0.rearrange("(p t) j -> p t j", t=PACK)
+        out_words = out_1[0].rearrange("p n t -> p (n t)")
+
+        def scores(c):
+            h, c0 = divmod(c * CHUNK, HALF)
+            s = psum.tile([P, PACK, CHUNK], F32, name="s%d" % c)
+            for t in range(PACK):
+                nc.tensor.matmul_mx(
+                    out=s[:, t, :],
+                    lhsT=d_word[:, t * P : (t + 1) * P].bitcast(FP8X4),
+                    lhsT_scale=d_scale[:, t * P : (t + 1) * P],
+                    rhs=x_word[h][:, c0 : c0 + CHUNK].bitcast(FP8X4),
+                    rhs_scale=x_scale[h][:, c0 : c0 + CHUNK],
+                    start=True,
+                    stop=True,
+                )
+            pos = keep.tile([P, CHUNK, PACK], F32, name="pos%d" % c)
+            nc.scalar.activation(pos[:], s[:].rearrange("p t j -> p j t"), ACT.Relu)
+            sq = keep.tile([P, CHUNK, PACK], F32, name="sq%d" % c)
+            nc.scalar.activation(sq[:], pos[:], ACT.Square)
+            z = keep.tile([P, CHUNK, PACK], BF16, name="z%d" % c, align_bytes=64)
+            nc.vector.tensor_tensor(z[:], sq[:], gain[:].unsqueeze(1).broadcast_to([P, CHUNK, PACK]), MULT)
+            nc.vector.quantize_mx(out=z_word[c][:].bitcast(FP8X4), scales=z_scale[c][:], in_=z[:].rearrange("p j t -> p (j t)"))
+
+        def values(c):
+            cols = slice(c * CHUNK, (c + 1) * CHUNK)
+            acc = psum.tile([P, PACK, CHUNK], F32, name="acc%d" % c)
+            for t in range(PACK):
+                nc.tensor.matmul_mx(
+                    out=acc[:, t, :],
+                    lhsT=w_word[:, 2 * t * P : 2 * (t + 1) * P].bitcast(FP4X4),
+                    lhsT_scale=w_scale[:, t * P : (t + 1) * P],
+                    rhs=z_word[c][:].bitcast(FP8X4),
+                    rhs_scale=z_scale[c][:],
+                    start=True,
+                    stop=True,
+                )
+            y = keep.tile([P, PACK, CHUNK], F32, name="y%d" % c)
+            nc.vector.tensor_tensor(y[:], acc[:], factor[:, cols].unsqueeze(1).broadcast_to([P, PACK, CHUNK]), MULT)
+            nc.sync.dma_start(out_rows[:, :, cols], y[:])
+            yb = keep.tile([P, CHUNK, PACK], BF16, name="yb%d" % c, align_bytes=64)
+            weave = nc.vector.tensor_copy if c == CHUNKS - 1 else nc.scalar.copy
+            weave(yb[:].rearrange("p (a i) t -> p a t i", i=4), y[:].rearrange("p t (a i) -> p a t i", i=4))
+            nc.vector.quantize_mx(out=y_word[:, cols].bitcast(FP8X4), scales=y_scale[:, cols], in_=yb[:].rearrange("p j t -> p (j t)"))
+            if c % 2 == 1:
+                first = (c - 1) * CHUNK
+                nc.sync.dma_start(out_words[:, 4 * first : 4 * (first + HALF)].bitcast(I32), y_word[:, first : first + HALF].bitcast(I32))
+
+        gather_queries(0)
+        scores(0)
+        gather_queries(1)
+        deal_weights()
+        for c in range(1, CHUNKS):
+            scores(c)
+        for c in range(CHUNKS):
+            values(c)
+        for q in range(4):
+            queue = nc.scalar if q % 2 == 0 else nc.sync
+            queue.dma_start(out_2[0][4 * q : 4 * q + 4, :].bitcast(I32), y_scale[32 * q : 32 * q + 4, :].bitcast(I32))

@@ -28,61 +28,54 @@ def tile_picked_reluattn_relu_po_kernel(tc, x_words, x_scales, d_words, d_scales
     with ExitStack() as ctx:
         lists = ctx.enter_context(tc.tile_pool(name="lists", bufs=1))
         keep = ctx.enter_context(tc.tile_pool(name="keep", bufs=1))
-        reuse = ctx.enter_context(tc.tile_pool(name="reuse", bufs=1))
         psum = ctx.enter_context(tc.psum_pool(name="psum", bufs=1))
 
         key_list = lists.tile([P, ENTRIES // 16], U16, name="key_list")
         query_list = lists.tile([P, ENTRIES // 16], U16, name="query_list")
-        nc.sync.dma_start(key_list[:], kidx)
-        nc.sync.dma_start(query_list[:], offs)
-        gain_raw = keep.tile([P, PACK], F32, name="gain_raw")
-        nc.sync.dma_start(gain_raw[:], gn.rearrange("(p t) o -> p (t o)", t=PACK))
-
+        d_scale_table = keep.tile([P, TABLE], U8, name="d_scale_table", align_bytes=64)
+        x_scale_table = keep.tile([P, TABLE], U8, name="x_scale_table", align_bytes=64)
         d_word_table = keep.tile([P, TABLE], I32, name="d_word_table", align_bytes=64)
         x_word_table = keep.tile([P, TABLE], I32, name="x_word_table", align_bytes=64)
-        nc.sync.dma_start(d_word_table[:], d_words[0].rearrange("p n t -> p (n t)").bitcast(I32))
-        nc.sync.dma_start(x_word_table[:], x_words[0].rearrange("p n t -> p (n t)").bitcast(I32))
-
-        d_scale_table = reuse.tile([P, TABLE], U8, name="d_scale_table", align_bytes=64, offset=0)
-        x_scale_table = keep.tile([P, TABLE], U8, name="x_scale_table", align_bytes=64)
+        w_word_raw = keep.tile([P, 2 * ENTRIES], U8, name="w_word_raw", align_bytes=64)
         w_scale_raw = keep.tile([P, ENTRIES], U8, name="w_scale_raw", align_bytes=64)
-        nc.gpsimd.memset(d_scale_table[:].bitcast(I32), 0)
+        gain = keep.tile([P, PACK], F32, name="gain")
+        factor = keep.tile([P, ENTRIES], F32, name="factor")
+
         nc.vector.memset(x_scale_table[:].bitcast(I32), 0)
         nc.gpsimd.memset(w_scale_raw[:].bitcast(I32), 0)
-        for v in range(2):
-            nc.scalar.dma_start(d_scale_table[v:P:16, :].bitcast(I32), d_scales[0][v:16:2, :].bitcast(I32))
+        nc.sync.dma_start(key_list[:], kidx)
+        nc.sync.dma_start(d_scale_table[:].bitcast(I32), d_scales[0].bitcast(I32).unsqueeze(1).broadcast_to([16, 8, TABLE // 4]))
+        nc.sync.dma_start(query_list[:], offs)
         for q in range(4):
-            nc.scalar.dma_start(x_scale_table[32 * q : 32 * q + 4, :].bitcast(I32), x_scales[0][4 * q : 4 * q + 4, :].bitcast(I32))
+            queue = nc.sync if q < 2 else nc.scalar
+            queue.dma_start(x_scale_table[32 * q : 32 * q + 4, :].bitcast(I32), x_scales[0][4 * q : 4 * q + 4, :].bitcast(I32))
+        nc.sync.dma_start(d_word_table[:], d_words[0].rearrange("p n t -> p (n t)").bitcast(I32))
+        nc.sync.dma_start(x_word_table[:], x_words[0].rearrange("p n t -> p (n t)").bitcast(I32))
+        nc.sync.dma_start(gain[:], gn.rearrange("(p t) o -> p (t o)", t=PACK))
+        nc.sync.dma_start(w_word_raw[:].bitcast(I32), w1_words[0].bitcast(I32))
         for q in range(4):
-            nc.gpsimd.dma_start(w_scale_raw[32 * q : 32 * q + 4, :].bitcast(I32), w1_scales[0][4 * q : 4 * q + 4, :].bitcast(I32))
+            nc.sync.dma_start(w_scale_raw[32 * q : 32 * q + 4, :].bitcast(I32), w1_scales[0][4 * q : 4 * q + 4, :].bitcast(I32))
+        nc.sync.dma_start(factor[:], cnt)
 
-        gain = keep.tile([P, PACK], F32, name="gain")
-        nc.scalar.activation(gain[:], gain_raw[:], ACT.Copy, scale=0.0625 * 0.0625)
-
-        d_scale_picked = reuse.tile([P, ENTRIES], U8, name="d_scale_picked", align_bytes=64, offset=4096)
+        d_scale_picked = keep.tile([P, ENTRIES], U8, name="d_scale_picked", align_bytes=64)
         d_scale = keep.tile([P, ENTRIES], U8, name="d_scale", align_bytes=64)
         nc.vector.tensor_copy(d_scale_picked[:], d_scale_table[:].indirect(key_list[:]))
         nc.vector.tensor_copy(d_scale[:].rearrange("p (t m) -> p t m", t=PACK), d_scale_picked[:].rearrange("p (m t) -> p t m", t=PACK))
+        for b in range(1, 4):
+            nc.scalar.dma_start(d_scale[b:P:32, :].bitcast(I32), d_scale[8 * b : P : 32, :].bitcast(I32))
 
-        w_word_raw = reuse.tile([P, 2 * ENTRIES], U8, name="w_word_raw", align_bytes=64, offset=0)
-        factor = reuse.tile([P, ENTRIES], F32, name="factor", align_bytes=64, offset=1024)
-        nc.sync.dma_start(w_word_raw[:].bitcast(I32), w1_words[0].bitcast(I32))
-        nc.sync.dma_start(factor[:], cnt)
+        x_scale = keep.tile([P, ENTRIES], U8, name="x_scale", align_bytes=64)
+        nc.vector.tensor_copy(x_scale[:], x_scale_table[:].indirect(query_list[:]))
 
-        for v in range(2):
-            nc.scalar.dma_start(d_scale[2 + v : P : 32, :].bitcast(I32), d_scale[16 + v : P : 32, :].bitcast(I32))
-
-        d_word_picked = reuse.tile([P, ENTRIES], U32, name="d_word_picked", align_bytes=64, offset=4096)
+        d_word_picked = keep.tile([P, ENTRIES], U32, name="d_word_picked", align_bytes=64)
         d_word = keep.tile([P, ENTRIES], U32, name="d_word", align_bytes=64)
         nc.vector.tensor_copy(d_word_picked[:], d_word_table[:].bitcast(U32).indirect(key_list[:]))
         nc.vector.tensor_copy(d_word[:].rearrange("p (t m) -> p m t", t=PACK), d_word_picked[:].rearrange("p (m t) -> p m t", t=PACK))
 
         x_word = [keep.tile([P, HALF], U32, name="x_word%d" % h, align_bytes=64) for h in range(2)]
-        x_scale = [keep.tile([P, HALF], U8, name="x_scale%d" % h, align_bytes=64) for h in range(2)]
 
         def gather_queries(h):
             piece = query_list[:, h * HALF // 16 : (h + 1) * HALF // 16]
-            nc.vector.tensor_copy(x_scale[h][:], x_scale_table[:].indirect(piece))
             nc.vector.tensor_copy(x_word[h][:], x_word_table[:].bitcast(U32).indirect(piece))
 
         w_word = keep.tile([P, 2 * ENTRIES], U8, name="w_word", align_bytes=64)
@@ -108,12 +101,12 @@ def tile_picked_reluattn_relu_po_kernel(tc, x_words, x_scales, d_words, d_scales
                     lhsT=d_word[:, t * P : (t + 1) * P].bitcast(FP8X4),
                     lhsT_scale=d_scale[:, t * P : (t + 1) * P],
                     rhs=x_word[h][:, c0 : c0 + CHUNK].bitcast(FP8X4),
-                    rhs_scale=x_scale[h][:, c0 : c0 + CHUNK],
+                    rhs_scale=x_scale[:, c * CHUNK : (c + 1) * CHUNK],
                     start=True,
                     stop=True,
                 )
             pos = keep.tile([P, CHUNK, PACK], F32, name="pos%d" % c)
-            nc.scalar.activation(pos[:], s[:].rearrange("p t j -> p j t"), ACT.Relu)
+            nc.scalar.activation(pos[:], s[:].rearrange("p t j -> p j t"), ACT.Relu, scale=0.0625)
             sq = keep.tile([P, CHUNK, PACK], F32, name="sq%d" % c)
             nc.scalar.activation(sq[:], pos[:], ACT.Square)
             z = keep.tile([P, CHUNK, PACK], BF16, name="z%d" % c, align_bytes=64)
@@ -145,8 +138,8 @@ def tile_picked_reluattn_relu_po_kernel(tc, x_words, x_scales, d_words, d_scales
                 nc.sync.dma_start(out_words[:, 4 * first : 4 * (first + HALF)].bitcast(I32), y_word[:, first : first + HALF].bitcast(I32))
 
         gather_queries(0)
-        scores(0)
         gather_queries(1)
+        scores(0)
         deal_weights()
         for c in range(1, CHUNKS):
             scores(c)

@@ -12,6 +12,7 @@ FP8X4 = mybir.dt.float8_e4m3fn_x4
 FP4X4 = mybir.dt.float4_e2m1fn_x4
 ACT = mybir.ActivationFunctionType
 MULT = mybir.AluOpType.mult
+MAX = mybir.AluOpType.max
 
 P = 128
 PACK = 4
@@ -32,30 +33,29 @@ def tile_picked_reluattn_relu_po_kernel(tc, x_words, x_scales, d_words, d_scales
 
         key_list = lists.tile([P, ENTRIES // 16], U16, name="key_list")
         query_list = lists.tile([P, ENTRIES // 16], U16, name="query_list")
-        d_scale_table = keep.tile([P, TABLE], U8, name="d_scale_table", align_bytes=64)
+        d_scale_table = keep.tile([P, TABLE], U8, name="d_scale_table", tag="scale_rows", align_bytes=64)
         x_scale_table = keep.tile([P, TABLE], U8, name="x_scale_table", align_bytes=64)
         d_word_table = keep.tile([P, TABLE], I32, name="d_word_table", align_bytes=64)
         x_word_table = keep.tile([P, TABLE], I32, name="x_word_table", align_bytes=64)
         w_word_raw = keep.tile([P, 2 * ENTRIES], U8, name="w_word_raw", align_bytes=64)
-        w_scale_raw = keep.tile([P, ENTRIES], U8, name="w_scale_raw", align_bytes=64)
         gain = keep.tile([P, PACK], F32, name="gain")
         factor = keep.tile([P, ENTRIES], F32, name="factor")
 
         nc.vector.memset(x_scale_table[:].bitcast(I32), 0)
-        nc.gpsimd.memset(w_scale_raw[:].bitcast(I32), 0)
         nc.sync.dma_start(key_list[:], kidx)
         nc.sync.dma_start(d_scale_table[:].bitcast(I32), d_scales[0].bitcast(I32).unsqueeze(1).broadcast_to([16, 8, TABLE // 4]))
         nc.sync.dma_start(query_list[:], offs)
         for q in range(4):
             queue = nc.sync if q < 2 else nc.scalar
-            queue.dma_start(x_scale_table[32 * q : 32 * q + 4, :].bitcast(I32), x_scales[0][4 * q : 4 * q + 4, :].bitcast(I32))
+            queue.dma_start(x_scale_table[32 * q + 4 : 32 * q + 8, :].bitcast(I32), x_scales[0][4 * q : 4 * q + 4, :].bitcast(I32))
         nc.sync.dma_start(d_word_table[:], d_words[0].rearrange("p n t -> p (n t)").bitcast(I32))
         nc.sync.dma_start(x_word_table[:], x_words[0].rearrange("p n t -> p (n t)").bitcast(I32))
-        nc.sync.dma_start(gain[:], gn.rearrange("(p t) o -> p (t o)", t=PACK))
+        nc.gpsimd.dma_start(gain[:], gn.rearrange("(p t) o -> p (t o)", t=PACK))
         nc.sync.dma_start(w_word_raw[:].bitcast(I32), w1_words[0].bitcast(I32))
-        for q in range(4):
-            nc.sync.dma_start(w_scale_raw[32 * q : 32 * q + 4, :].bitcast(I32), w1_scales[0][4 * q : 4 * q + 4, :].bitcast(I32))
         nc.sync.dma_start(factor[:], cnt)
+
+        gain_scaled = keep.tile([P, PACK], F32, name="gain_scaled")
+        nc.scalar.activation(gain_scaled[:], gain[:], ACT.Copy, scale=0.0625 * 0.0625)
 
         d_scale_picked = keep.tile([P, ENTRIES], U8, name="d_scale_picked", align_bytes=64)
         d_scale = keep.tile([P, ENTRIES], U8, name="d_scale", align_bytes=64)
@@ -63,6 +63,11 @@ def tile_picked_reluattn_relu_po_kernel(tc, x_words, x_scales, d_words, d_scales
         nc.vector.tensor_copy(d_scale[:].rearrange("p (t m) -> p t m", t=PACK), d_scale_picked[:].rearrange("p (m t) -> p t m", t=PACK))
         for b in range(1, 4):
             nc.scalar.dma_start(d_scale[b:P:32, :].bitcast(I32), d_scale[8 * b : P : 32, :].bitcast(I32))
+
+        w_scale_raw = keep.tile([P, ENTRIES], U8, name="w_scale_raw", tag="scale_rows", align_bytes=64)
+        nc.gpsimd.memset(w_scale_raw[:].bitcast(I32), 0)
+        for q in range(4):
+            nc.scalar.dma_start(w_scale_raw[32 * q : 32 * q + 4, :].bitcast(I32), w1_scales[0][4 * q : 4 * q + 4, :].bitcast(I32))
 
         x_scale = keep.tile([P, ENTRIES], U8, name="x_scale", align_bytes=64)
         nc.vector.tensor_copy(x_scale[:], x_scale_table[:].indirect(query_list[:]))
@@ -101,16 +106,15 @@ def tile_picked_reluattn_relu_po_kernel(tc, x_words, x_scales, d_words, d_scales
                     lhsT=d_word[:, t * P : (t + 1) * P].bitcast(FP8X4),
                     lhsT_scale=d_scale[:, t * P : (t + 1) * P],
                     rhs=x_word[h][:, c0 : c0 + CHUNK].bitcast(FP8X4),
-                    rhs_scale=x_scale[:, c * CHUNK : (c + 1) * CHUNK],
+                    rhs_scale=x_scale[4:P, c * CHUNK : (c + 1) * CHUNK],
                     start=True,
                     stop=True,
                 )
-            pos = keep.tile([P, CHUNK, PACK], F32, name="pos%d" % c)
-            nc.scalar.activation(pos[:], s[:].rearrange("p t j -> p j t"), ACT.Relu, scale=0.0625)
-            sq = keep.tile([P, CHUNK, PACK], F32, name="sq%d" % c)
-            nc.scalar.activation(sq[:], pos[:], ACT.Square)
+            u = keep.tile([P, PACK, CHUNK], F32, name="u%d" % c)
+            for t in range(PACK):
+                nc.scalar.activation(u[:, t, :], s[:, t, :], ACT.Copy, scale=gain_scaled[:, t : t + 1])
             z = keep.tile([P, CHUNK, PACK], BF16, name="z%d" % c, align_bytes=64)
-            nc.vector.tensor_tensor(z[:], sq[:], gain[:].unsqueeze(1).broadcast_to([P, CHUNK, PACK]), MULT)
+            nc.vector.scalar_tensor_tensor(z[:], s[:].rearrange("p t j -> p j t"), 0.0, u[:].rearrange("p t j -> p j t"), MAX, MULT)
             nc.vector.quantize_mx(out=z_word[c][:].bitcast(FP8X4), scales=z_scale[c][:], in_=z[:].rearrange("p j t -> p (j t)"))
 
         def values(c):
@@ -139,9 +143,8 @@ def tile_picked_reluattn_relu_po_kernel(tc, x_words, x_scales, d_words, d_scales
 
         gather_queries(0)
         gather_queries(1)
-        scores(0)
         deal_weights()
-        for c in range(1, CHUNKS):
+        for c in range(CHUNKS):
             scores(c)
         for c in range(CHUNKS):
             values(c)

@@ -87,7 +87,7 @@ def tile_picked_reluattn_relu_po_kernel(tc, x_words, x_scales, d_words, d_scales
         w_scale = keep.tile([P, ENTRIES], U8, name="w_scale", align_bytes=64)
 
         def deal_weights():
-            nc.vector.tensor_copy(w_word[:].rearrange("p (t m b) -> p t m b", t=PACK, b=2), w_word_raw[:].rearrange("p (m t b) -> p t m b", t=PACK, b=2))
+            nc.vector.tensor_copy(w_word[:].bitcast(U16).rearrange("p (t m) -> p t m", t=PACK), w_word_raw[:].bitcast(U16).rearrange("p (m t) -> p t m", t=PACK))
             nc.vector.tensor_copy(w_scale[:].rearrange("p (t m) -> p t m", t=PACK), w_scale_raw[:].rearrange("p (m t) -> p t m", t=PACK))
 
         z_word = [keep.tile([P, CHUNK], U32, name="z_word%d" % c, align_bytes=64) for c in range(CHUNKS)]
@@ -96,6 +96,8 @@ def tile_picked_reluattn_relu_po_kernel(tc, x_words, x_scales, d_words, d_scales
         y_scale = keep.tile([P, ENTRIES], U8, name="y_scale", align_bytes=64)
         out_rows = out_0.rearrange("(p t) j -> p t j", t=PACK)
         out_words = out_1[0].rearrange("p n t -> p (n t)")
+
+        s_bank, u_tile, z_tile, acc_bank, y_tile, yb_tile = {}, {}, {}, {}, {}, {}
 
         def scores(c):
             h, c0 = divmod(c * CHUNK, HALF)
@@ -110,15 +112,18 @@ def tile_picked_reluattn_relu_po_kernel(tc, x_words, x_scales, d_words, d_scales
                     start=True,
                     stop=True,
                 )
-            u = keep.tile([P, PACK, CHUNK], F32, name="u%d" % c)
+            u = keep.tile([P, PACK, CHUNK + 1], F32, name="u%d" % c)
             for t in range(PACK):
-                nc.scalar.activation(u[:, t, :], s[:, t, :], ACT.Copy, scale=gain_scaled[:, t : t + 1])
+                nc.scalar.activation(u[:, t, :CHUNK], s[:, t, :], ACT.Copy, scale=gain_scaled[:, t : t + 1])
+            s_bank[c], u_tile[c] = s, u
+
+        def weights(c):
             z = keep.tile([P, CHUNK, PACK], BF16, name="z%d" % c, align_bytes=64)
-            nc.vector.scalar_tensor_tensor(z[:], s[:].rearrange("p t j -> p j t"), 0.0, u[:].rearrange("p t j -> p j t"), MAX, MULT)
-            nc.vector.quantize_mx(out=z_word[c][:].bitcast(FP8X4), scales=z_scale[c][:], in_=z[:].rearrange("p j t -> p (j t)"))
+            nc.vector.scalar_tensor_tensor(z[:], s_bank[c][:].rearrange("p t j -> p j t"), 0.0, u_tile[c][:, :, :CHUNK].rearrange("p t j -> p j t"), MAX, MULT)
+            z_tile[c] = z
 
         def values(c):
-            cols = slice(c * CHUNK, (c + 1) * CHUNK)
+            nc.vector.quantize_mx(out=z_word[c][:].bitcast(FP8X4), scales=z_scale[c][:], in_=z_tile[c][:].rearrange("p j t -> p (j t)"))
             acc = psum.tile([P, PACK, CHUNK], F32, name="acc%d" % c)
             for t in range(PACK):
                 nc.tensor.matmul_mx(
@@ -130,13 +135,24 @@ def tile_picked_reluattn_relu_po_kernel(tc, x_words, x_scales, d_words, d_scales
                     start=True,
                     stop=True,
                 )
+            acc_bank[c] = acc
+
+        def result(c):
+            cols = slice(c * CHUNK, (c + 1) * CHUNK)
             y = keep.tile([P, PACK, CHUNK], F32, name="y%d" % c)
-            nc.vector.tensor_tensor(y[:], acc[:], factor[:, cols].unsqueeze(1).broadcast_to([P, PACK, CHUNK]), MULT)
+            nc.vector.tensor_tensor(y[:], acc_bank[c][:], factor[:, cols].unsqueeze(1).broadcast_to([P, PACK, CHUNK]), MULT)
             nc.sync.dma_start(out_rows[:, :, cols], y[:])
+            y_tile[c] = y
+
+        def weave(c):
             yb = keep.tile([P, CHUNK, PACK], BF16, name="yb%d" % c, align_bytes=64)
-            weave = nc.vector.tensor_copy if c == CHUNKS - 1 else nc.scalar.copy
-            weave(yb[:].rearrange("p (a i) t -> p a t i", i=4), y[:].rearrange("p t (a i) -> p a t i", i=4))
-            nc.vector.quantize_mx(out=y_word[:, cols].bitcast(FP8X4), scales=y_scale[:, cols], in_=yb[:].rearrange("p j t -> p (j t)"))
+            copy = nc.vector.tensor_copy if c == CHUNKS - 1 else nc.scalar.copy
+            copy(yb[:].rearrange("p (a i) t -> p a t i", i=4), y_tile[c][:].rearrange("p t (a i) -> p a t i", i=4))
+            yb_tile[c] = yb
+
+        def planes(c):
+            cols = slice(c * CHUNK, (c + 1) * CHUNK)
+            nc.vector.quantize_mx(out=y_word[:, cols].bitcast(FP8X4), scales=y_scale[:, cols], in_=yb_tile[c][:].rearrange("p j t -> p (j t)"))
             if c % 2 == 1:
                 first = (c - 1) * CHUNK
                 nc.sync.dma_start(out_words[:, 4 * first : 4 * (first + HALF)].bitcast(I32), y_word[:, first : first + HALF].bitcast(I32))
@@ -147,7 +163,12 @@ def tile_picked_reluattn_relu_po_kernel(tc, x_words, x_scales, d_words, d_scales
         for c in range(CHUNKS):
             scores(c)
         for c in range(CHUNKS):
+            weights(c)
             values(c)
+        for c in range(CHUNKS):
+            result(c)
+            weave(c)
+            planes(c)
         for q in range(4):
             queue = nc.scalar if q % 2 == 0 else nc.sync
             queue.dma_start(out_2[0][4 * q : 4 * q + 4, :].bitcast(I32), y_scale[32 * q : 32 * q + 4, :].bitcast(I32))

@@ -35,11 +35,10 @@ def tile_picked_reluattn_relu_po_kernel(tc, x_words, x_scales, d_words, d_scales
         query_list = lists.tile([P, ENTRIES // 16], U16, name="query_list")
         d_scale_table = keep.tile([P, TABLE], U8, name="d_scale_table", tag="scale_rows", align_bytes=64)
         x_scale_table = keep.tile([P, TABLE], U8, name="x_scale_table", align_bytes=64)
-        d_word_table = keep.tile([P, TABLE], I32, name="d_word_table", align_bytes=64)
+        d_word_table = keep.tile([P, TABLE], I32, name="d_word_table", tag="key_words", align_bytes=64)
         x_word_table = keep.tile([P, TABLE], I32, name="x_word_table", align_bytes=64)
         w_word_raw = keep.tile([P, 2 * ENTRIES], U8, name="w_word_raw", align_bytes=64)
         gain = keep.tile([P, PACK], F32, name="gain")
-        factor = keep.tile([P, ENTRIES], F32, name="factor")
 
         nc.vector.memset(x_scale_table[:].bitcast(I32), 0)
         nc.sync.dma_start(key_list[:], kidx)
@@ -50,9 +49,8 @@ def tile_picked_reluattn_relu_po_kernel(tc, x_words, x_scales, d_words, d_scales
             queue.dma_start(x_scale_table[32 * q + 4 : 32 * q + 8, :].bitcast(I32), x_scales[0][4 * q : 4 * q + 4, :].bitcast(I32))
         nc.sync.dma_start(d_word_table[:], d_words[0].rearrange("p n t -> p (n t)").bitcast(I32))
         nc.sync.dma_start(x_word_table[:], x_words[0].rearrange("p n t -> p (n t)").bitcast(I32))
-        nc.gpsimd.dma_start(gain[:], gn.rearrange("(p t) o -> p (t o)", t=PACK))
         nc.sync.dma_start(w_word_raw[:].bitcast(I32), w1_words[0].bitcast(I32))
-        nc.sync.dma_start(factor[:], cnt)
+        nc.sync.dma_start(gain[:], gn.rearrange("(p t) o -> p (t o)", t=PACK))
 
         gain_scaled = keep.tile([P, PACK], F32, name="gain_scaled")
         nc.scalar.activation(gain_scaled[:], gain[:], ACT.Copy, scale=0.0625 * 0.0625)
@@ -67,7 +65,7 @@ def tile_picked_reluattn_relu_po_kernel(tc, x_words, x_scales, d_words, d_scales
         w_scale_raw = keep.tile([P, ENTRIES], U8, name="w_scale_raw", tag="scale_rows", align_bytes=64)
         nc.gpsimd.memset(w_scale_raw[:].bitcast(I32), 0)
         for q in range(4):
-            nc.scalar.dma_start(w_scale_raw[32 * q : 32 * q + 4, :].bitcast(I32), w1_scales[0][4 * q : 4 * q + 4, :].bitcast(I32))
+            nc.sync.dma_start(w_scale_raw[32 * q : 32 * q + 4, :].bitcast(I32), w1_scales[0][4 * q : 4 * q + 4, :].bitcast(I32))
 
         x_scale = keep.tile([P, ENTRIES], U8, name="x_scale", align_bytes=64)
         nc.vector.tensor_copy(x_scale[:], x_scale_table[:].indirect(query_list[:]))
@@ -76,6 +74,9 @@ def tile_picked_reluattn_relu_po_kernel(tc, x_words, x_scales, d_words, d_scales
         d_word = keep.tile([P, ENTRIES], U32, name="d_word", align_bytes=64)
         nc.vector.tensor_copy(d_word_picked[:], d_word_table[:].bitcast(U32).indirect(key_list[:]))
         nc.vector.tensor_copy(d_word[:].rearrange("p (t m) -> p m t", t=PACK), d_word_picked[:].rearrange("p (m t) -> p m t", t=PACK))
+
+        factor = keep.tile([P, ENTRIES], F32, name="factor", tag="key_words", align_bytes=64)
+        nc.sync.dma_start(factor[:], cnt)
 
         x_word = [keep.tile([P, HALF], U32, name="x_word%d" % h, align_bytes=64) for h in range(2)]
 
@@ -112,14 +113,14 @@ def tile_picked_reluattn_relu_po_kernel(tc, x_words, x_scales, d_words, d_scales
                     start=True,
                     stop=True,
                 )
-            u = keep.tile([P, PACK, CHUNK + 1], F32, name="u%d" % c)
+            u = keep.tile([P, PACK, CHUNK], F32, name="u%d" % c)
             for t in range(PACK):
-                nc.scalar.activation(u[:, t, :CHUNK], s[:, t, :], ACT.Copy, scale=gain_scaled[:, t : t + 1])
+                nc.scalar.activation(u[:, t, :], s[:, t, :], ACT.Copy, scale=gain_scaled[:, t : t + 1])
             s_bank[c], u_tile[c] = s, u
 
         def weights(c):
             z = keep.tile([P, CHUNK, PACK], BF16, name="z%d" % c, align_bytes=64)
-            nc.vector.scalar_tensor_tensor(z[:], s_bank[c][:].rearrange("p t j -> p j t"), 0.0, u_tile[c][:, :, :CHUNK].rearrange("p t j -> p j t"), MAX, MULT)
+            nc.vector.scalar_tensor_tensor(z[:], s_bank[c][:].rearrange("p t j -> p j t"), 0.0, u_tile[c][:].rearrange("p t j -> p j t"), MAX, MULT)
             z_tile[c] = z
 
         def values(c):

@@ -21,6 +21,7 @@ ENTRIES = 512
 CHUNK = 128
 CHUNKS = ENTRIES // CHUNK
 HALF = 256
+SCALED = 3
 FLOPS = 2 * 2 * 512 * 512 * 512
 
 
@@ -38,7 +39,7 @@ def tile_picked_reluattn_relu_po_kernel(tc, x_words, x_scales, d_words, d_scales
         d_word_table = keep.tile([P, TABLE], I32, name="d_word_table", tag="key_words", align_bytes=64)
         x_word_table = keep.tile([P, TABLE], I32, name="x_word_table", align_bytes=64)
         w_word_raw = keep.tile([P, 2 * ENTRIES], U8, name="w_word_raw", align_bytes=64)
-        gain = keep.tile([P, PACK], F32, name="gain")
+        gain = keep.tile([P, PACK], F32, name="gain", tag="r%d" % (CHUNKS - 1))
 
         nc.vector.memset(x_scale_table[:].bitcast(I32), 0)
         nc.sync.dma_start(key_list[:], kidx)
@@ -113,14 +114,23 @@ def tile_picked_reluattn_relu_po_kernel(tc, x_words, x_scales, d_words, d_scales
                     start=True,
                     stop=True,
                 )
-            u = keep.tile([P, PACK, CHUNK], F32, name="u%d" % c)
-            for t in range(PACK):
-                nc.scalar.activation(u[:, t, :], s[:, t, :], ACT.Copy, scale=gain_scaled[:, t : t + 1])
+            if c < SCALED:
+                u = keep.tile([P, PACK, CHUNK], F32, name="u%d" % c)
+                for t in range(PACK):
+                    nc.scalar.activation(u[:, t, :], s[:, t, :], ACT.Copy, scale=gain_scaled[:, t : t + 1])
+            else:
+                r = keep.tile([P, CHUNK, PACK], F32, name="r%d" % c, tag="r%d" % c)
+                nc.scalar.activation(r[:], s[:].rearrange("p t j -> p j t"), ACT.Relu)
+                u = keep.tile([P, CHUNK, PACK], F32, name="u%d" % c)
+                nc.scalar.activation(u[:], r[:], ACT.Square)
             s_bank[c], u_tile[c] = s, u
 
         def weights(c):
             z = keep.tile([P, CHUNK, PACK], BF16, name="z%d" % c, align_bytes=64)
-            nc.vector.scalar_tensor_tensor(z[:], s_bank[c][:].rearrange("p t j -> p j t"), 0.0, u_tile[c][:].rearrange("p t j -> p j t"), MAX, MULT)
+            if c < SCALED:
+                nc.vector.scalar_tensor_tensor(z[:], s_bank[c][:].rearrange("p t j -> p j t"), 0.0, u_tile[c][:].rearrange("p t j -> p j t"), MAX, MULT)
+            else:
+                nc.vector.tensor_tensor(z[:], u_tile[c][:], gain_scaled[:].unsqueeze(1).broadcast_to([P, CHUNK, PACK]), MULT)
             z_tile[c] = z
 
         def values(c):
@@ -138,17 +148,21 @@ def tile_picked_reluattn_relu_po_kernel(tc, x_words, x_scales, d_words, d_scales
                 )
             acc_bank[c] = acc
 
+        middle = []
+
         def result(c):
             cols = slice(c * CHUNK, (c + 1) * CHUNK)
-            y = keep.tile([P, PACK, CHUNK], F32, name="y%d" % c)
-            nc.vector.tensor_tensor(y[:], acc_bank[c][:], factor[:, cols].unsqueeze(1).broadcast_to([P, PACK, CHUNK]), MULT)
-            nc.sync.dma_start(out_rows[:, :, cols], y[:])
+            if c == 1:
+                middle.append(keep.tile([P, 2, PACK, CHUNK], F32, name="y_middle", tag="r%d" % (CHUNKS - 1)))
+            y = middle[0][:, c - 1] if c in (1, 2) else keep.tile([P, PACK, CHUNK], F32, name="y%d" % c)[:]
+            nc.vector.tensor_tensor(y, acc_bank[c][:], factor[:, cols].unsqueeze(1).broadcast_to([P, PACK, CHUNK]), MULT)
+            nc.sync.dma_start(out_rows[:, :, cols], y)
             y_tile[c] = y
 
         def weave(c):
             yb = keep.tile([P, CHUNK, PACK], BF16, name="yb%d" % c, align_bytes=64)
             copy = nc.vector.tensor_copy if c == CHUNKS - 1 else nc.scalar.copy
-            copy(yb[:].rearrange("p (a i) t -> p a t i", i=4), y_tile[c][:].rearrange("p t (a i) -> p a t i", i=4))
+            copy(yb[:].rearrange("p (a i) t -> p a t i", i=4), y_tile[c].rearrange("p t (a i) -> p a t i", i=4))
             yb_tile[c] = yb
 
         def planes(c):
@@ -165,11 +179,18 @@ def tile_picked_reluattn_relu_po_kernel(tc, x_words, x_scales, d_words, d_scales
             scores(c)
         for c in range(CHUNKS):
             weights(c)
+            if c >= 2:
+                result(c - 2)
             values(c)
-        for c in range(CHUNKS):
-            result(c)
+        result(2)
+        for c in range(CHUNKS - 1):
             weave(c)
-            planes(c)
+        planes(0)
+        planes(1)
+        result(CHUNKS - 1)
+        planes(2)
+        weave(CHUNKS - 1)
+        planes(CHUNKS - 1)
         for q in range(4):
             queue = nc.scalar if q % 2 == 0 else nc.sync
             queue.dma_start(out_2[0][4 * q : 4 * q + 4, :].bitcast(I32), y_scale[32 * q : 32 * q + 4, :].bitcast(I32))

@@ -90,6 +90,8 @@ def tile_picked_reluattn_relu_po_kernel(tc, x_words, x_scales, d_words, d_scales
 
         def deal_weights():
             nc.vector.tensor_copy(w_word[:].bitcast(U16).rearrange("p (t m) -> p t m", t=PACK), w_word_raw[:].bitcast(U16).rearrange("p (m t) -> p t m", t=PACK))
+
+        def deal_weight_scales():
             nc.vector.tensor_copy(w_scale[:].rearrange("p (t m) -> p t m", t=PACK), w_scale_raw[:].rearrange("p (m t) -> p t m", t=PACK))
 
         z_word = [keep.tile([P, CHUNK], U32, name="z_word%d" % c, align_bytes=64) for c in range(CHUNKS)]
@@ -114,7 +116,11 @@ def tile_picked_reluattn_relu_po_kernel(tc, x_words, x_scales, d_words, d_scales
                     start=True,
                     stop=True,
                 )
-            if c < SCALED:
+            if c == 0:
+                u = keep.tile([P, CHUNK, PACK], F32, name="u%d" % c)
+                nc.vector.tensor_tensor(u[:], s[:].rearrange("p t j -> p j t"), gain_scaled[:].unsqueeze(1).broadcast_to([P, CHUNK, PACK]), MULT)
+                deal_weight_scales()
+            elif c < SCALED:
                 u = keep.tile([P, PACK, CHUNK], F32, name="u%d" % c)
                 for t in range(PACK):
                     nc.scalar.activation(u[:, t, :], s[:, t, :], ACT.Copy, scale=gain_scaled[:, t : t + 1])
@@ -127,7 +133,9 @@ def tile_picked_reluattn_relu_po_kernel(tc, x_words, x_scales, d_words, d_scales
 
         def weights(c):
             z = keep.tile([P, CHUNK, PACK], BF16, name="z%d" % c, align_bytes=64)
-            if c < SCALED:
+            if c == 0:
+                nc.vector.scalar_tensor_tensor(z[:], s_bank[c][:].rearrange("p t j -> p j t"), 0.0, u_tile[c][:], MAX, MULT)
+            elif c < SCALED:
                 nc.vector.scalar_tensor_tensor(z[:], s_bank[c][:].rearrange("p t j -> p j t"), 0.0, u_tile[c][:].rearrange("p t j -> p j t"), MAX, MULT)
             else:
                 nc.vector.tensor_tensor(z[:], u_tile[c][:], gain_scaled[:].unsqueeze(1).broadcast_to([P, CHUNK, PACK]), MULT)

@@ -34,42 +34,43 @@ def tile_picked_reluattn_relu_po_kernel(tc, x_words, x_scales, d_words, d_scales
 
         key_list = lists.tile([P, ENTRIES // 16], U16, name="key_list")
         query_list = lists.tile([P, ENTRIES // 16], U16, name="query_list")
-        d_scale_table = keep.tile([P, TABLE], U8, name="d_scale_table", tag="scale_rows", align_bytes=64)
+        d_scale_table = keep.tile([P, TABLE], U8, name="d_scale_table", align_bytes=64)
+        w_scale_raw = keep.tile([P, ENTRIES], U8, name="w_scale_raw", align_bytes=64)
         x_scale_table = keep.tile([P, TABLE], U8, name="x_scale_table", align_bytes=64)
-        d_word_table = keep.tile([P, TABLE], I32, name="d_word_table", tag="key_words", align_bytes=64)
-        x_word_table = keep.tile([P, TABLE], I32, name="x_word_table", align_bytes=64)
+        d_word_table = keep.tile([P, TABLE], I32, name="d_word_table", align_bytes=64)
+        x_word_table = keep.tile([P, TABLE], I32, name="x_word_table", tag="key_words", align_bytes=64)
         w_word_raw = keep.tile([P, 2 * ENTRIES], U8, name="w_word_raw", align_bytes=64)
         gain = keep.tile([P, PACK], F32, name="gain", tag="r%d" % (CHUNKS - 1))
 
+        nc.vector.memset(d_scale_table[:].bitcast(I32), 0)
         nc.vector.memset(x_scale_table[:].bitcast(I32), 0)
+        nc.vector.memset(w_scale_raw[:].bitcast(I32), 0)
+        nc.scalar.dma_start(gain[:], gn.rearrange("(p t) o -> p (t o)", t=PACK))
         nc.sync.dma_start(key_list[:], kidx)
-        nc.sync.dma_start(d_scale_table[:].bitcast(I32), d_scales[0].bitcast(I32).unsqueeze(1).broadcast_to([16, 8, TABLE // 4]))
         nc.sync.dma_start(query_list[:], offs)
-        for q in range(4):
-            queue = nc.sync if q < 2 else nc.scalar
-            queue.dma_start(x_scale_table[32 * q + 4 : 32 * q + 8, :].bitcast(I32), x_scales[0][4 * q : 4 * q + 4, :].bitcast(I32))
+        nc.sync.dma_start(d_scale_table[0:P:8, :].bitcast(I32), d_scales[0].bitcast(I32))
+        nc.sync.dma_start(x_scale_table[0:P:8, :].bitcast(I32), x_scales[0].bitcast(I32))
+        nc.sync.dma_start(w_scale_raw[0:P:8, :].bitcast(I32), w1_scales[0].bitcast(I32))
         nc.sync.dma_start(d_word_table[:], d_words[0].rearrange("p n t -> p (n t)").bitcast(I32))
         nc.sync.dma_start(x_word_table[:], x_words[0].rearrange("p n t -> p (n t)").bitcast(I32))
         nc.sync.dma_start(w_word_raw[:].bitcast(I32), w1_words[0].bitcast(I32))
-        nc.sync.dma_start(gain[:], gn.rearrange("(p t) o -> p (t o)", t=PACK))
 
         gain_scaled = keep.tile([P, PACK], F32, name="gain_scaled")
         nc.scalar.activation(gain_scaled[:], gain[:], ACT.Copy, scale=0.0625 * 0.0625)
 
         d_scale_picked = keep.tile([P, ENTRIES], U8, name="d_scale_picked", align_bytes=64)
-        d_scale = keep.tile([P, ENTRIES], U8, name="d_scale", align_bytes=64)
+        x_scale_picked = keep.tile([P, ENTRIES], U8, name="x_scale_picked", align_bytes=64)
+        scale_planes = keep.tile([P, 3 * ENTRIES], U8, name="scale_planes", align_bytes=64)
+        d_scale = scale_planes[:, 0:ENTRIES]
+        x_scale = scale_planes[:, ENTRIES : 2 * ENTRIES]
+        w_scale = scale_planes[:, 2 * ENTRIES : 3 * ENTRIES]
         nc.vector.tensor_copy(d_scale_picked[:], d_scale_table[:].indirect(key_list[:]))
-        nc.vector.tensor_copy(d_scale[:].rearrange("p (t m) -> p t m", t=PACK), d_scale_picked[:].rearrange("p (m t) -> p t m", t=PACK))
+        nc.vector.tensor_copy(x_scale_picked[:], x_scale_table[:].indirect(query_list[:]))
+        nc.vector.tensor_copy(d_scale.rearrange("p (t m) -> p t m", t=PACK), d_scale_picked[:].rearrange("p (m t) -> p t m", t=PACK))
+        nc.vector.tensor_copy(w_scale.rearrange("p (t m) -> p t m", t=PACK), w_scale_raw[:].rearrange("p (m t) -> p t m", t=PACK))
+        nc.vector.tensor_copy(x_scale.bitcast(I32), x_scale_picked[:].bitcast(I32))
         for b in range(1, 4):
-            nc.scalar.dma_start(d_scale[b:P:32, :].bitcast(I32), d_scale[8 * b : P : 32, :].bitcast(I32))
-
-        w_scale_raw = keep.tile([P, ENTRIES], U8, name="w_scale_raw", tag="scale_rows", align_bytes=64)
-        nc.gpsimd.memset(w_scale_raw[:].bitcast(I32), 0)
-        for q in range(4):
-            nc.sync.dma_start(w_scale_raw[32 * q : 32 * q + 4, :].bitcast(I32), w1_scales[0][4 * q : 4 * q + 4, :].bitcast(I32))
-
-        x_scale = keep.tile([P, ENTRIES], U8, name="x_scale", align_bytes=64)
-        nc.vector.tensor_copy(x_scale[:], x_scale_table[:].indirect(query_list[:]))
+            nc.scalar.dma_start(scale_planes[b:P:32, :].bitcast(I32), scale_planes[8 * b : P : 32, :].bitcast(I32))
 
         d_word_picked = keep.tile([P, ENTRIES], U32, name="d_word_picked", align_bytes=64)
         d_word = keep.tile([P, ENTRIES], U32, name="d_word", align_bytes=64)
@@ -86,13 +87,9 @@ def tile_picked_reluattn_relu_po_kernel(tc, x_words, x_scales, d_words, d_scales
             nc.vector.tensor_copy(x_word[h][:], x_word_table[:].bitcast(U32).indirect(piece))
 
         w_word = keep.tile([P, 2 * ENTRIES], U8, name="w_word", align_bytes=64)
-        w_scale = keep.tile([P, ENTRIES], U8, name="w_scale", align_bytes=64)
 
         def deal_weights():
             nc.vector.tensor_copy(w_word[:].bitcast(U16).rearrange("p (t m) -> p t m", t=PACK), w_word_raw[:].bitcast(U16).rearrange("p (m t) -> p t m", t=PACK))
-
-        def deal_weight_scales():
-            nc.vector.tensor_copy(w_scale[:].rearrange("p (t m) -> p t m", t=PACK), w_scale_raw[:].rearrange("p (m t) -> p t m", t=PACK))
 
         z_word = [keep.tile([P, CHUNK], U32, name="z_word%d" % c, align_bytes=64) for c in range(CHUNKS)]
         z_scale = [keep.tile([P, CHUNK], U8, name="z_scale%d" % c, align_bytes=64) for c in range(CHUNKS)]
@@ -112,14 +109,13 @@ def tile_picked_reluattn_relu_po_kernel(tc, x_words, x_scales, d_words, d_scales
                     lhsT=d_word[:, t * P : (t + 1) * P].bitcast(FP8X4),
                     lhsT_scale=d_scale[:, t * P : (t + 1) * P],
                     rhs=x_word[h][:, c0 : c0 + CHUNK].bitcast(FP8X4),
-                    rhs_scale=x_scale[4:P, c * CHUNK : (c + 1) * CHUNK],
+                    rhs_scale=x_scale[:, c * CHUNK : (c + 1) * CHUNK],
                     start=True,
                     stop=True,
                 )
             if c == 0:
                 u = keep.tile([P, CHUNK, PACK], F32, name="u%d" % c)
                 nc.vector.tensor_tensor(u[:], s[:].rearrange("p t j -> p j t"), gain_scaled[:].unsqueeze(1).broadcast_to([P, CHUNK, PACK]), MULT)
-                deal_weight_scales()
             elif c < SCALED:
                 u = keep.tile([P, PACK, CHUNK], F32, name="u%d" % c)
                 for t in range(PACK):

@@ -21,7 +21,7 @@ ENTRIES = 512
 CHUNK = 128
 CHUNKS = ENTRIES // CHUNK
 HALF = 256
-SCALED = 3
+SCORE_SCALE = 0.0625
 FLOPS = 2 * 2 * 512 * 512 * 512
 
 
@@ -36,46 +36,58 @@ def tile_picked_reluattn_relu_po_kernel(tc, x_words, x_scales, d_words, d_scales
         query_list = lists.tile([P, ENTRIES // 16], U16, name="query_list")
         d_scale_table = keep.tile([P, TABLE], U8, name="d_scale_table", align_bytes=64)
         w_scale_raw = keep.tile([P, ENTRIES], U8, name="w_scale_raw", align_bytes=64)
-        x_scale_table = keep.tile([P, TABLE], U8, name="x_scale_table", align_bytes=64)
+        x_scale_table = keep.tile([P, TABLE], U8, name="x_scale_table", tag="query_scales", align_bytes=64)
         d_word_table = keep.tile([P, TABLE], I32, name="d_word_table", align_bytes=64)
         x_word_table = keep.tile([P, TABLE], I32, name="x_word_table", tag="key_words", align_bytes=64)
         w_word_raw = keep.tile([P, 2 * ENTRIES], U8, name="w_word_raw", align_bytes=64)
-        gain = keep.tile([P, PACK], F32, name="gain", tag="r%d" % (CHUNKS - 1))
+        gain = keep.tile([P, PACK], F32, name="gain", align_bytes=64)
 
-        nc.vector.memset(d_scale_table[:].bitcast(I32), 0)
         nc.vector.memset(x_scale_table[:].bitcast(I32), 0)
-        nc.vector.memset(w_scale_raw[:].bitcast(I32), 0)
+        nc.scalar.dma_start(w_scale_raw[:].bitcast(I32), w1_scales[0].bitcast(I32).unsqueeze(1).broadcast_to([16, 8, ENTRIES // 4]))
         nc.scalar.dma_start(gain[:], gn.rearrange("(p t) o -> p (t o)", t=PACK))
         nc.sync.dma_start(key_list[:], kidx)
+        nc.sync.dma_start(d_scale_table[:].bitcast(I32), d_scales[0].bitcast(I32).unsqueeze(1).broadcast_to([16, 8, TABLE // 4]))
         nc.sync.dma_start(query_list[:], offs)
-        nc.sync.dma_start(d_scale_table[0:P:8, :].bitcast(I32), d_scales[0].bitcast(I32))
         nc.sync.dma_start(x_scale_table[0:P:8, :].bitcast(I32), x_scales[0].bitcast(I32))
-        nc.sync.dma_start(w_scale_raw[0:P:8, :].bitcast(I32), w1_scales[0].bitcast(I32))
         nc.sync.dma_start(d_word_table[:], d_words[0].rearrange("p n t -> p (n t)").bitcast(I32))
         nc.sync.dma_start(x_word_table[:], x_words[0].rearrange("p n t -> p (n t)").bitcast(I32))
         nc.sync.dma_start(w_word_raw[:].bitcast(I32), w1_words[0].bitcast(I32))
 
-        gain_scaled = keep.tile([P, PACK], F32, name="gain_scaled")
-        nc.scalar.activation(gain_scaled[:], gain[:], ACT.Copy, scale=0.0625 * 0.0625)
+        gain_size = keep.tile([P, PACK], F32, name="gain_size", tag="gain_size")
+        gain_root = keep.tile([P, PACK], F32, name="gain_root")
+        gain_sign = keep.tile([P, CHUNK, PACK], BF16, name="gain_sign", align_bytes=64)
+        nc.vector.scalar_tensor_tensor(gain_size[:], gain[:], -1.0, gain[:], MULT, MAX)
+        nc.scalar.activation(gain_root[:], gain_size[:], ACT.Sqrt, scale=SCORE_SCALE * SCORE_SCALE)
+        gain_scaled = keep.tile([P, PACK], F32, name="gain_scaled", tag="gain_size")
+        nc.scalar.activation(gain_scaled[:], gain[:], ACT.Copy, scale=SCORE_SCALE * SCORE_SCALE)
+        nc.scalar.activation(gain_sign[:], gain_scaled[:].unsqueeze(1).broadcast_to([P, CHUNK, PACK]), ACT.Sign)
+
+        def move_rows(plane):
+            for b in range(1, 4):
+                nc.scalar.dma_start(plane[b:P:32, :].bitcast(I32), plane[8 * b : P : 32, :].bitcast(I32))
+
+        w_scale = keep.tile([P, ENTRIES], U8, name="w_scale", align_bytes=64)
+        nc.vector.tensor_copy(w_scale[:].rearrange("p (t m) -> p t m", t=PACK), w_scale_raw[:].rearrange("p (m t) -> p t m", t=PACK))
+        move_rows(w_scale)
 
         d_scale_picked = keep.tile([P, ENTRIES], U8, name="d_scale_picked", align_bytes=64)
         x_scale_picked = keep.tile([P, ENTRIES], U8, name="x_scale_picked", align_bytes=64)
-        scale_planes = keep.tile([P, 3 * ENTRIES], U8, name="scale_planes", align_bytes=64)
-        d_scale = scale_planes[:, 0:ENTRIES]
-        x_scale = scale_planes[:, ENTRIES : 2 * ENTRIES]
-        w_scale = scale_planes[:, 2 * ENTRIES : 3 * ENTRIES]
         nc.vector.tensor_copy(d_scale_picked[:], d_scale_table[:].indirect(key_list[:]))
         nc.vector.tensor_copy(x_scale_picked[:], x_scale_table[:].indirect(query_list[:]))
+        scale_planes = keep.tile([P, 2 * ENTRIES], U8, name="scale_planes", tag="query_scales", align_bytes=64)
+        d_scale = scale_planes[:, 0:ENTRIES]
+        x_scale = scale_planes[:, ENTRIES : 2 * ENTRIES]
         nc.vector.tensor_copy(d_scale.rearrange("p (t m) -> p t m", t=PACK), d_scale_picked[:].rearrange("p (m t) -> p t m", t=PACK))
-        nc.vector.tensor_copy(w_scale.rearrange("p (t m) -> p t m", t=PACK), w_scale_raw[:].rearrange("p (m t) -> p t m", t=PACK))
         nc.vector.tensor_copy(x_scale.bitcast(I32), x_scale_picked[:].bitcast(I32))
-        for b in range(1, 4):
-            nc.scalar.dma_start(scale_planes[b:P:32, :].bitcast(I32), scale_planes[8 * b : P : 32, :].bitcast(I32))
+        move_rows(scale_planes)
 
-        d_word_picked = keep.tile([P, ENTRIES], U32, name="d_word_picked", align_bytes=64)
+        d_word_picked = [keep.tile([P, HALF], U32, name="d_word_picked%d" % h, align_bytes=64) for h in range(2)]
         d_word = keep.tile([P, ENTRIES], U32, name="d_word", align_bytes=64)
-        nc.vector.tensor_copy(d_word_picked[:], d_word_table[:].bitcast(U32).indirect(key_list[:]))
-        nc.vector.tensor_copy(d_word[:].rearrange("p (t m) -> p m t", t=PACK), d_word_picked[:].rearrange("p (m t) -> p m t", t=PACK))
+        for h in range(2):
+            nc.vector.tensor_copy(d_word_picked[h][:], d_word_table[:].bitcast(U32).indirect(key_list[:, h * HALF // 16 : (h + 1) * HALF // 16]))
+        for h in range(2):
+            dealt = d_word[:].rearrange("p (t m) -> p m t", t=PACK)[:, h * HALF // PACK : (h + 1) * HALF // PACK, :]
+            nc.vector.tensor_copy(dealt, d_word_picked[h][:].rearrange("p (m t) -> p m t", t=PACK))
 
         factor = keep.tile([P, ENTRIES], F32, name="factor", tag="key_words", align_bytes=64)
         nc.sync.dma_start(factor[:], cnt)
@@ -100,6 +112,12 @@ def tile_picked_reluattn_relu_po_kernel(tc, x_words, x_scales, d_words, d_scales
 
         s_bank, u_tile, z_tile, acc_bank, y_tile, yb_tile = {}, {}, {}, {}, {}, {}
 
+        def in_fours(woven):
+            return woven.rearrange("p (a i) t -> p a t i", i=4)
+
+        def from_fours(slots):
+            return slots.rearrange("p t (a i) -> p a t i", i=4)
+
         def scores(c):
             h, c0 = divmod(c * CHUNK, HALF)
             s = psum.tile([P, PACK, CHUNK], F32, name="s%d" % c)
@@ -113,28 +131,35 @@ def tile_picked_reluattn_relu_po_kernel(tc, x_words, x_scales, d_words, d_scales
                     start=True,
                     stop=True,
                 )
-            if c == 0:
-                u = keep.tile([P, CHUNK, PACK], F32, name="u%d" % c)
-                nc.vector.tensor_tensor(u[:], s[:].rearrange("p t j -> p j t"), gain_scaled[:].unsqueeze(1).broadcast_to([P, CHUNK, PACK]), MULT)
-            elif c < SCALED:
-                u = keep.tile([P, PACK, CHUNK], F32, name="u%d" % c)
-                for t in range(PACK):
-                    nc.scalar.activation(u[:, t, :], s[:, t, :], ACT.Copy, scale=gain_scaled[:, t : t + 1])
-            else:
-                r = keep.tile([P, CHUNK, PACK], F32, name="r%d" % c, tag="r%d" % c)
-                nc.scalar.activation(r[:], s[:].rearrange("p t j -> p j t"), ACT.Relu)
-                u = keep.tile([P, CHUNK, PACK], F32, name="u%d" % c)
-                nc.scalar.activation(u[:], r[:], ACT.Square)
-            s_bank[c], u_tile[c] = s, u
+            s_bank[c] = s
 
-        def weights(c):
+        def factor_on_vector(c):
+            u = keep.tile([P, CHUNK, PACK], F32, name="u%d" % c)
+            nc.vector.tensor_tensor(u[:], s_bank[c][:].rearrange("p t j -> p j t"), gain_scaled[:].unsqueeze(1).broadcast_to([P, CHUNK, PACK]), MULT)
+            u_tile[c] = u[:]
+
+        def factor_on_scalar(c):
+            u = keep.tile([P, PACK, CHUNK], F32, name="u%d" % c)
+            for t in range(PACK):
+                nc.scalar.activation(u[:, t, :], s_bank[c][:, t, :], ACT.Copy, scale=gain_scaled[:, t : t + 1])
+            u_tile[c] = u[:].rearrange("p t j -> p j t")
+
+        def product(c):
             z = keep.tile([P, CHUNK, PACK], BF16, name="z%d" % c, align_bytes=64)
-            if c == 0:
-                nc.vector.scalar_tensor_tensor(z[:], s_bank[c][:].rearrange("p t j -> p j t"), 0.0, u_tile[c][:], MAX, MULT)
-            elif c < SCALED:
-                nc.vector.scalar_tensor_tensor(z[:], s_bank[c][:].rearrange("p t j -> p j t"), 0.0, u_tile[c][:].rearrange("p t j -> p j t"), MAX, MULT)
-            else:
-                nc.vector.tensor_tensor(z[:], u_tile[c][:], gain_scaled[:].unsqueeze(1).broadcast_to([P, CHUNK, PACK]), MULT)
+            nc.vector.scalar_tensor_tensor(z[:], s_bank[c][:].rearrange("p t j -> p j t"), 0.0, u_tile[c], MAX, MULT)
+            z_tile[c] = z
+
+        def size_on_scalar(c):
+            r = keep.tile([P, PACK, CHUNK], F32, name="r%d" % c, tag="r%d" % c, align_bytes=64)
+            for t in range(PACK):
+                nc.scalar.activation(r[:, t, :], s_bank[c][:, t, :], ACT.Relu, scale=gain_root[:, t : t + 1])
+            u = keep.tile([P, CHUNK, PACK], BF16, name="u%d" % c, align_bytes=64)
+            nc.scalar.activation(in_fours(u[:]), from_fours(r[:]), ACT.Square)
+            u_tile[c] = u[:]
+
+        def signed(c):
+            z = keep.tile([P, CHUNK, PACK], BF16, name="z%d" % c, align_bytes=64)
+            nc.vector.tensor_tensor(z[:], u_tile[c], gain_sign[:], MULT)
             z_tile[c] = z
 
         def values(c):
@@ -152,21 +177,16 @@ def tile_picked_reluattn_relu_po_kernel(tc, x_words, x_scales, d_words, d_scales
                 )
             acc_bank[c] = acc
 
-        middle = []
-
         def result(c):
             cols = slice(c * CHUNK, (c + 1) * CHUNK)
-            if c == 1:
-                middle.append(keep.tile([P, 2, PACK, CHUNK], F32, name="y_middle", tag="r%d" % (CHUNKS - 1)))
-            y = middle[0][:, c - 1] if c in (1, 2) else keep.tile([P, PACK, CHUNK], F32, name="y%d" % c)[:]
-            nc.vector.tensor_tensor(y, acc_bank[c][:], factor[:, cols].unsqueeze(1).broadcast_to([P, PACK, CHUNK]), MULT)
-            nc.sync.dma_start(out_rows[:, :, cols], y)
+            y = keep.tile([P, PACK, CHUNK], F32, name="y%d" % c)
+            nc.vector.tensor_tensor(y[:], acc_bank[c][:], factor[:, cols].unsqueeze(1).broadcast_to([P, PACK, CHUNK]), MULT)
+            nc.sync.dma_start(out_rows[:, :, cols], y[:])
             y_tile[c] = y
 
-        def weave(c):
-            yb = keep.tile([P, CHUNK, PACK], BF16, name="yb%d" % c, align_bytes=64)
-            copy = nc.vector.tensor_copy if c == CHUNKS - 1 else nc.scalar.copy
-            copy(yb[:].rearrange("p (a i) t -> p a t i", i=4), y_tile[c].rearrange("p t (a i) -> p a t i", i=4))
+        def weave(c, copy):
+            yb = keep.tile([P, CHUNK, PACK], BF16, name="yb%d" % c, tag="r%d" % (CHUNKS - 1 - c), align_bytes=64)
+            copy(in_fours(yb[:]), from_fours(y_tile[c][:]))
             yb_tile[c] = yb
 
         def planes(c):
@@ -178,23 +198,33 @@ def tile_picked_reluattn_relu_po_kernel(tc, x_words, x_scales, d_words, d_scales
 
         gather_queries(0)
         gather_queries(1)
-        deal_weights()
         for c in range(CHUNKS):
             scores(c)
-        for c in range(CHUNKS):
-            weights(c)
-            if c >= 2:
-                result(c - 2)
-            values(c)
+        factor_on_vector(0)
+        deal_weights()
+        factor_on_scalar(1)
+        factor_on_scalar(2)
+        size_on_scalar(3)
+        product(0)
+        product(1)
+        values(0)
+        product(2)
+        values(1)
+        result(0)
+        signed(3)
+        values(2)
+        values(3)
+        result(1)
         result(2)
-        for c in range(CHUNKS - 1):
-            weave(c)
+        weave(0, nc.scalar.copy)
+        weave(1, nc.scalar.copy)
+        weave(2, nc.scalar.copy)
         planes(0)
+        result(3)
         planes(1)
-        result(CHUNKS - 1)
+        weave(3, nc.vector.tensor_copy)
         planes(2)
-        weave(CHUNKS - 1)
-        planes(CHUNKS - 1)
+        planes(3)
         for q in range(4):
             queue = nc.scalar if q % 2 == 0 else nc.sync
             queue.dma_start(out_2[0][4 * q : 4 * q + 4, :].bitcast(I32), y_scale[32 * q : 32 * q + 4, :].bitcast(I32))

@@ -21,6 +21,7 @@ ENTRIES = 512
 CHUNK = 128
 CHUNKS = ENTRIES // CHUNK
 HALF = 256
+EARLY = 512
 SCORE_SCALE = 0.0625
 FLOPS = 2 * 2 * 512 * 512 * 512
 
@@ -42,14 +43,17 @@ def tile_picked_reluattn_relu_po_kernel(tc, x_words, x_scales, d_words, d_scales
         w_word_raw = keep.tile([P, 2 * ENTRIES], U8, name="w_word_raw", align_bytes=64)
         gain = keep.tile([P, PACK], F32, name="gain", align_bytes=64)
 
+        d_word_rows = d_words[0].rearrange("p n t -> p (n t)").bitcast(I32)
+        nc.vector.memset(d_scale_table[:].bitcast(I32), 0)
         nc.vector.memset(x_scale_table[:].bitcast(I32), 0)
         nc.scalar.dma_start(w_scale_raw[:].bitcast(I32), w1_scales[0].bitcast(I32).unsqueeze(1).broadcast_to([16, 8, ENTRIES // 4]))
         nc.scalar.dma_start(gain[:], gn.rearrange("(p t) o -> p (t o)", t=PACK))
+        nc.sync.dma_start(d_word_table[:, :EARLY], d_word_rows[:, :EARLY])
         nc.sync.dma_start(key_list[:], kidx)
-        nc.sync.dma_start(d_scale_table[:].bitcast(I32), d_scales[0].bitcast(I32).unsqueeze(1).broadcast_to([16, 8, TABLE // 4]))
         nc.sync.dma_start(query_list[:], offs)
+        nc.sync.dma_start(d_scale_table[0:P:8, :].bitcast(I32), d_scales[0].bitcast(I32))
         nc.sync.dma_start(x_scale_table[0:P:8, :].bitcast(I32), x_scales[0].bitcast(I32))
-        nc.sync.dma_start(d_word_table[:], d_words[0].rearrange("p n t -> p (n t)").bitcast(I32))
+        nc.sync.dma_start(d_word_table[:, EARLY:], d_word_rows[:, EARLY:])
         nc.sync.dma_start(x_word_table[:], x_words[0].rearrange("p n t -> p (n t)").bitcast(I32))
         nc.sync.dma_start(w_word_raw[:].bitcast(I32), w1_words[0].bitcast(I32))
 

@@ -46,13 +46,14 @@ def tile_picked_reluattn_relu_po_kernel(tc, x_words, x_scales, d_words, d_scales
         d_word_rows = d_words[0].rearrange("p n t -> p (n t)").bitcast(I32)
         nc.vector.memset(d_scale_table[:].bitcast(I32), 0)
         nc.vector.memset(x_scale_table[:].bitcast(I32), 0)
-        nc.scalar.dma_start(w_scale_raw[:].bitcast(I32), w1_scales[0].bitcast(I32).unsqueeze(1).broadcast_to([16, 8, ENTRIES // 4]))
+        nc.vector.memset(w_scale_raw[:].bitcast(I32), 0)
         nc.scalar.dma_start(gain[:], gn.rearrange("(p t) o -> p (t o)", t=PACK))
         nc.sync.dma_start(d_word_table[:, :EARLY], d_word_rows[:, :EARLY])
         nc.sync.dma_start(key_list[:], kidx)
         nc.sync.dma_start(query_list[:], offs)
         nc.sync.dma_start(d_scale_table[0:P:8, :].bitcast(I32), d_scales[0].bitcast(I32))
         nc.sync.dma_start(x_scale_table[0:P:8, :].bitcast(I32), x_scales[0].bitcast(I32))
+        nc.sync.dma_start(w_scale_raw[0:P:8, :].bitcast(I32), w1_scales[0].bitcast(I32))
         nc.sync.dma_start(d_word_table[:, EARLY:], d_word_rows[:, EARLY:])
         nc.sync.dma_start(x_word_table[:], x_words[0].rearrange("p n t -> p (n t)").bitcast(I32))
         nc.sync.dma_start(w_word_raw[:].bitcast(I32), w1_words[0].bitcast(I32))
@@ -70,18 +71,16 @@ def tile_picked_reluattn_relu_po_kernel(tc, x_words, x_scales, d_words, d_scales
             for b in range(1, 4):
                 nc.scalar.dma_start(plane[b:P:32, :].bitcast(I32), plane[8 * b : P : 32, :].bitcast(I32))
 
-        w_scale = keep.tile([P, ENTRIES], U8, name="w_scale", align_bytes=64)
-        nc.vector.tensor_copy(w_scale[:].rearrange("p (t m) -> p t m", t=PACK), w_scale_raw[:].rearrange("p (m t) -> p t m", t=PACK))
-        move_rows(w_scale)
-
         d_scale_picked = keep.tile([P, ENTRIES], U8, name="d_scale_picked", align_bytes=64)
         x_scale_picked = keep.tile([P, ENTRIES], U8, name="x_scale_picked", align_bytes=64)
         nc.vector.tensor_copy(d_scale_picked[:], d_scale_table[:].indirect(key_list[:]))
         nc.vector.tensor_copy(x_scale_picked[:], x_scale_table[:].indirect(query_list[:]))
-        scale_planes = keep.tile([P, 2 * ENTRIES], U8, name="scale_planes", tag="query_scales", align_bytes=64)
+        scale_planes = keep.tile([P, 3 * ENTRIES], U8, name="scale_planes", tag="query_scales", align_bytes=64)
         d_scale = scale_planes[:, 0:ENTRIES]
         x_scale = scale_planes[:, ENTRIES : 2 * ENTRIES]
         nc.vector.tensor_copy(d_scale.rearrange("p (t m) -> p t m", t=PACK), d_scale_picked[:].rearrange("p (m t) -> p t m", t=PACK))
+        w_scale = scale_planes[:, 2 * ENTRIES : 3 * ENTRIES]
+        nc.vector.tensor_copy(w_scale.rearrange("p (t m) -> p t m", t=PACK), w_scale_raw[:].rearrange("p (m t) -> p t m", t=PACK))
         nc.vector.tensor_copy(x_scale.bitcast(I32), x_scale_picked[:].bitcast(I32))
         move_rows(scale_planes)
 

@@ -21,7 +21,6 @@ ENTRIES = 512
 CHUNK = 128
 CHUNKS = ENTRIES // CHUNK
 HALF = 256
-EARLY = 512
 SCORE_SCALE = 0.0625
 FLOPS = 2 * 2 * 512 * 512 * 512
 
@@ -48,13 +47,12 @@ def tile_picked_reluattn_relu_po_kernel(tc, x_words, x_scales, d_words, d_scales
         nc.vector.memset(x_scale_table[:].bitcast(I32), 0)
         nc.vector.memset(w_scale_raw[:].bitcast(I32), 0)
         nc.scalar.dma_start(gain[:], gn.rearrange("(p t) o -> p (t o)", t=PACK))
-        nc.sync.dma_start(d_word_table[:, :EARLY], d_word_rows[:, :EARLY])
         nc.sync.dma_start(key_list[:], kidx)
         nc.sync.dma_start(query_list[:], offs)
         nc.sync.dma_start(d_scale_table[0:P:8, :].bitcast(I32), d_scales[0].bitcast(I32))
         nc.sync.dma_start(x_scale_table[0:P:8, :].bitcast(I32), x_scales[0].bitcast(I32))
         nc.sync.dma_start(w_scale_raw[0:P:8, :].bitcast(I32), w1_scales[0].bitcast(I32))
-        nc.sync.dma_start(d_word_table[:, EARLY:], d_word_rows[:, EARLY:])
+        nc.sync.dma_start(d_word_table[:], d_word_rows)
         nc.sync.dma_start(x_word_table[:], x_words[0].rearrange("p n t -> p (n t)").bitcast(I32))
         nc.sync.dma_start(w_word_raw[:].bitcast(I32), w1_words[0].bitcast(I32))
 

@@ -45,32 +45,29 @@ def tile_picked_reluattn_relu_po_kernel(tc, x_words, x_scales, d_words, d_scales
         d_word_rows = d_words[0].rearrange("p n t -> p (n t)").bitcast(I32)
         nc.vector.memset(d_scale_table[:].bitcast(I32), 0)
         nc.vector.memset(x_scale_table[:].bitcast(I32), 0)
-        nc.vector.memset(w_scale_raw[:].bitcast(I32), 0)
+        nc.scalar.dma_start(w_scale_raw[:].bitcast(I32), w1_scales[0].bitcast(I32).unsqueeze(1).broadcast_to([16, 8, ENTRIES // 4]))
         nc.scalar.dma_start(gain[:], gn.rearrange("(p t) o -> p (t o)", t=PACK))
         nc.sync.dma_start(key_list[:], kidx)
         nc.sync.dma_start(query_list[:], offs)
         nc.sync.dma_start(d_scale_table[0:P:8, :].bitcast(I32), d_scales[0].bitcast(I32))
         nc.sync.dma_start(x_scale_table[0:P:8, :].bitcast(I32), x_scales[0].bitcast(I32))
-        nc.sync.dma_start(w_scale_raw[0:P:8, :].bitcast(I32), w1_scales[0].bitcast(I32))
         nc.sync.dma_start(d_word_table[:], d_word_rows)
         nc.sync.dma_start(x_word_table[:], x_words[0].rearrange("p n t -> p (n t)").bitcast(I32))
         nc.sync.dma_start(w_word_raw[:].bitcast(I32), w1_words[0].bitcast(I32))
 
-        gain_size = keep.tile([P, PACK], F32, name="gain_size", tag="gain_size")
+        gain_size = keep.tile([P, PACK], F32, name="gain_size")
         gain_root = keep.tile([P, PACK], F32, name="gain_root")
-        gain_sign = keep.tile([P, CHUNK, PACK], BF16, name="gain_sign", align_bytes=64)
-        nc.vector.scalar_tensor_tensor(gain_size[:], gain[:], -1.0, gain[:], MULT, MAX)
-        nc.scalar.activation(gain_root[:], gain_size[:], ACT.Sqrt, scale=SCORE_SCALE * SCORE_SCALE)
-        gain_scaled = keep.tile([P, PACK], F32, name="gain_scaled", tag="gain_size")
-        nc.scalar.activation(gain_scaled[:], gain[:], ACT.Copy, scale=SCORE_SCALE * SCORE_SCALE)
-        nc.scalar.activation(gain_sign[:], gain_scaled[:].unsqueeze(1).broadcast_to([P, CHUNK, PACK]), ACT.Sign)
+        nc.scalar.activation(gain_size[:], gain[:], ACT.Abs, scale=SCORE_SCALE * SCORE_SCALE)
+        nc.scalar.activation(gain_root[:], gain_size[:], ACT.Sqrt)
 
         def move_rows(plane):
             for b in range(1, 4):
                 nc.scalar.dma_start(plane[b:P:32, :].bitcast(I32), plane[8 * b : P : 32, :].bitcast(I32))
 
         d_scale_picked = keep.tile([P, ENTRIES], U8, name="d_scale_picked", align_bytes=64)
-        x_scale_picked = keep.tile([P, ENTRIES], U8, name="x_scale_picked", align_bytes=64)
+        x_scale_picked = keep.tile([P, ENTRIES], U8, name="x_scale_picked", tag="gain_scaled", align_bytes=64)
+        w_scale_dealt = keep.tile([P, ENTRIES], U8, name="w_scale_dealt", align_bytes=64)
+        nc.vector.tensor_copy(w_scale_dealt[:].rearrange("p (t m) -> p t m", t=PACK), w_scale_raw[:].rearrange("p (m t) -> p t m", t=PACK))
         nc.vector.tensor_copy(d_scale_picked[:], d_scale_table[:].indirect(key_list[:]))
         nc.vector.tensor_copy(x_scale_picked[:], x_scale_table[:].indirect(query_list[:]))
         scale_planes = keep.tile([P, 3 * ENTRIES], U8, name="scale_planes", tag="query_scales", align_bytes=64)
@@ -78,9 +75,14 @@ def tile_picked_reluattn_relu_po_kernel(tc, x_words, x_scales, d_words, d_scales
         x_scale = scale_planes[:, ENTRIES : 2 * ENTRIES]
         nc.vector.tensor_copy(d_scale.rearrange("p (t m) -> p t m", t=PACK), d_scale_picked[:].rearrange("p (m t) -> p t m", t=PACK))
         w_scale = scale_planes[:, 2 * ENTRIES : 3 * ENTRIES]
-        nc.vector.tensor_copy(w_scale.rearrange("p (t m) -> p t m", t=PACK), w_scale_raw[:].rearrange("p (m t) -> p t m", t=PACK))
+        nc.vector.tensor_copy(w_scale.bitcast(I32), w_scale_dealt[:].bitcast(I32))
         nc.vector.tensor_copy(x_scale.bitcast(I32), x_scale_picked[:].bitcast(I32))
         move_rows(scale_planes)
+
+        gain_scaled = keep.tile([P, PACK], F32, name="gain_scaled", tag="gain_scaled", align_bytes=64)
+        gain_sign = keep.tile([P, CHUNK, PACK], BF16, name="gain_sign", align_bytes=64)
+        nc.scalar.activation(gain_scaled[:], gain[:], ACT.Copy, scale=SCORE_SCALE * SCORE_SCALE)
+        nc.scalar.activation(gain_sign[:], gain_scaled[:].unsqueeze(1).broadcast_to([P, CHUNK, PACK]), ACT.Sign)
 
         d_word_picked = [keep.tile([P, HALF], U32, name="d_word_picked%d" % h, align_bytes=64) for h in range(2)]
         d_word = keep.tile([P, ENTRIES], U32, name="d_word", align_bytes=64)

@@ -136,9 +136,13 @@ def tile_picked_reluattn_relu_po_kernel(tc, x_words, x_scales, d_words, d_scales
                 )
             s_bank[c] = s
 
+        def halves(c, split):
+            return [slice(0, CHUNK // 2), slice(CHUNK // 2, CHUNK)] if split else [slice(0, CHUNK)]
+
         def factor_on_vector(c):
             u = keep.tile([P, CHUNK, PACK], F32, name="u%d" % c)
-            nc.vector.tensor_tensor(u[:], s_bank[c][:].rearrange("p t j -> p j t"), gain_scaled[:].unsqueeze(1).broadcast_to([P, CHUNK, PACK]), MULT)
+            for part in halves(c, True):
+                nc.vector.tensor_tensor(u[:, part, :], s_bank[c][:].rearrange("p t j -> p j t")[:, part, :], gain_scaled[:].unsqueeze(1).broadcast_to([P, CHUNK // 2, PACK]), MULT)
             u_tile[c] = u[:]
 
         def factor_on_scalar(c):
@@ -149,7 +153,8 @@ def tile_picked_reluattn_relu_po_kernel(tc, x_words, x_scales, d_words, d_scales
 
         def product(c):
             z = keep.tile([P, CHUNK, PACK], BF16, name="z%d" % c, align_bytes=64)
-            nc.vector.scalar_tensor_tensor(z[:], s_bank[c][:].rearrange("p t j -> p j t"), 0.0, u_tile[c], MAX, MULT)
+            for part in halves(c, c == 0):
+                nc.vector.scalar_tensor_tensor(z[:, part, :], s_bank[c][:].rearrange("p t j -> p j t")[:, part, :], 0.0, u_tile[c][:, part, :], MAX, MULT)
             z_tile[c] = z
 
         def size_on_scalar(c):
@@ -183,13 +188,16 @@ def tile_picked_reluattn_relu_po_kernel(tc, x_words, x_scales, d_words, d_scales
         def result(c):
             cols = slice(c * CHUNK, (c + 1) * CHUNK)
             y = keep.tile([P, PACK, CHUNK], F32, name="y%d" % c)
-            nc.vector.tensor_tensor(y[:], acc_bank[c][:], factor[:, cols].unsqueeze(1).broadcast_to([P, PACK, CHUNK]), MULT)
+            for part in halves(c, c == CHUNKS - 1):
+                width = part.stop - part.start
+                nc.vector.tensor_tensor(y[:, :, part], acc_bank[c][:, :, part], factor[:, cols][:, part].unsqueeze(1).broadcast_to([P, PACK, width]), MULT)
             nc.sync.dma_start(out_rows[:, :, cols], y[:])
             y_tile[c] = y
 
         def weave(c, copy):
             yb = keep.tile([P, CHUNK, PACK], BF16, name="yb%d" % c, tag="r%d" % (CHUNKS - 1 - c), align_bytes=64)
-            copy(in_fours(yb[:]), from_fours(y_tile[c][:]))
+            for part in halves(c, c == CHUNKS - 1):
+                copy(in_fours(yb[:, part, :]), from_fours(y_tile[c][:, :, part]))
             yb_tile[c] = yb
 
         def planes(c):

@@ -92,6 +92,18 @@ def tile_picked_reluattn_relu_po_kernel(tc, x_words, x_scales, d_words, d_scales
             dealt = d_word[:].rearrange("p (t m) -> p m t", t=PACK)[:, h * HALF // PACK : (h + 1) * HALF // PACK, :]
             nc.vector.tensor_copy(dealt, d_word_picked[h][:].rearrange("p (m t) -> p m t", t=PACK))
 
+        warm = psum.tile([P, ENTRIES], F32, name="warm", tag="acc%d" % (CHUNKS - 1))
+        for rep in range(2):
+            nc.tensor.matmul_mx(
+                out=warm[:],
+                lhsT=d_word_picked[0][:, :P].bitcast(FP8X4),
+                lhsT_scale=d_scale_picked[:, :P],
+                rhs=d_word_picked[0][:].bitcast(U8).bitcast(FP4X4),
+                rhs_scale=d_scale_picked[:],
+                start=True,
+                stop=True,
+            )
+
         factor = keep.tile([P, ENTRIES], F32, name="factor", tag="key_words", align_bytes=64)
         nc.sync.dma_start(factor[:], cnt)
 
@@ -172,7 +184,7 @@ def tile_picked_reluattn_relu_po_kernel(tc, x_words, x_scales, d_words, d_scales
 
         def values(c):
             nc.vector.quantize_mx(out=z_word[c][:].bitcast(FP8X4), scales=z_scale[c][:], in_=z_tile[c][:].rearrange("p j t -> p (j t)"))
-            acc = psum.tile([P, PACK, CHUNK], F32, name="acc%d" % c)
+            acc = psum.tile([P, PACK, CHUNK], F32, name="acc%d" % c, tag="acc%d" % c)
             for t in range(PACK):
                 nc.tensor.matmul_mx(
                     out=acc[:, t, :],

@@ -92,25 +92,13 @@ def tile_picked_reluattn_relu_po_kernel(tc, x_words, x_scales, d_words, d_scales
             dealt = d_word[:].rearrange("p (t m) -> p m t", t=PACK)[:, h * HALF // PACK : (h + 1) * HALF // PACK, :]
             nc.vector.tensor_copy(dealt, d_word_picked[h][:].rearrange("p (m t) -> p m t", t=PACK))
 
-        warm = psum.tile([P, ENTRIES], F32, name="warm", tag="acc%d" % (CHUNKS - 1))
-        for rep in range(2):
-            nc.tensor.matmul_mx(
-                out=warm[:],
-                lhsT=d_word_picked[0][:, :P].bitcast(FP8X4),
-                lhsT_scale=d_scale_picked[:, :P],
-                rhs=d_word_picked[0][:].bitcast(U8).bitcast(FP4X4),
-                rhs_scale=d_scale_picked[:],
-                start=True,
-                stop=True,
-            )
-
         factor = keep.tile([P, ENTRIES], F32, name="factor", tag="key_words", align_bytes=64)
         nc.sync.dma_start(factor[:], cnt)
 
-        x_word = [keep.tile([P, HALF], U32, name="x_word%d" % h, align_bytes=64) for h in range(2)]
+        x_word = [keep.tile([P, CHUNK], U32, name="x_word%d" % h, align_bytes=64) for h in range(CHUNKS)]
 
         def gather_queries(h):
-            piece = query_list[:, h * HALF // 16 : (h + 1) * HALF // 16]
+            piece = query_list[:, h * CHUNK // 16 : (h + 1) * CHUNK // 16]
             nc.vector.tensor_copy(x_word[h][:], x_word_table[:].bitcast(U32).indirect(piece))
 
         w_word = keep.tile([P, 2 * ENTRIES], U8, name="w_word", align_bytes=64)
@@ -134,14 +122,13 @@ def tile_picked_reluattn_relu_po_kernel(tc, x_words, x_scales, d_words, d_scales
             return slots.rearrange("p t (a i) -> p a t i", i=4)
 
         def scores(c):
-            h, c0 = divmod(c * CHUNK, HALF)
             s = psum.tile([P, PACK, CHUNK], F32, name="s%d" % c)
             for t in range(PACK):
                 nc.tensor.matmul_mx(
                     out=s[:, t, :],
                     lhsT=d_word[:, t * P : (t + 1) * P].bitcast(FP8X4),
                     lhsT_scale=d_scale[:, t * P : (t + 1) * P],
-                    rhs=x_word[h][:, c0 : c0 + CHUNK].bitcast(FP8X4),
+                    rhs=x_word[c][:].bitcast(FP8X4),
                     rhs_scale=x_scale[:, c * CHUNK : (c + 1) * CHUNK],
                     start=True,
                     stop=True,
@@ -151,12 +138,6 @@ def tile_picked_reluattn_relu_po_kernel(tc, x_words, x_scales, d_words, d_scales
         def halves(c, split):
             return [slice(0, CHUNK // 2), slice(CHUNK // 2, CHUNK)] if split else [slice(0, CHUNK)]
 
-        def factor_on_vector(c):
-            u = keep.tile([P, CHUNK, PACK], F32, name="u%d" % c)
-            for part in halves(c, True):
-                nc.vector.tensor_tensor(u[:, part, :], s_bank[c][:].rearrange("p t j -> p j t")[:, part, :], gain_scaled[:].unsqueeze(1).broadcast_to([P, CHUNK // 2, PACK]), MULT)
-            u_tile[c] = u[:]
-
         def factor_on_scalar(c):
             u = keep.tile([P, PACK, CHUNK], F32, name="u%d" % c)
             for t in range(PACK):
@@ -165,7 +146,7 @@ def tile_picked_reluattn_relu_po_kernel(tc, x_words, x_scales, d_words, d_scales
 
         def product(c):
             z = keep.tile([P, CHUNK, PACK], BF16, name="z%d" % c, align_bytes=64)
-            for part in halves(c, c == 0):
+            for part in halves(c, False):
                 nc.vector.scalar_tensor_tensor(z[:, part, :], s_bank[c][:].rearrange("p t j -> p j t")[:, part, :], 0.0, u_tile[c][:, part, :], MAX, MULT)
             z_tile[c] = z
 
@@ -219,12 +200,11 @@ def tile_picked_reluattn_relu_po_kernel(tc, x_words, x_scales, d_words, d_scales
                 first = (c - 1) * CHUNK
                 nc.sync.dma_start(out_words[:, 4 * first : 4 * (first + HALF)].bitcast(I32), y_word[:, first : first + HALF].bitcast(I32))
 
-        gather_queries(0)
-        gather_queries(1)
         for c in range(CHUNKS):
+            gather_queries(c)
             scores(c)
-        factor_on_vector(0)
         deal_weights()
+        factor_on_scalar(0)
         factor_on_scalar(1)
         factor_on_scalar(2)
         size_on_scalar(3)

@@ -73,7 +73,7 @@ def tile_picked_reluattn_relu_po_kernel(tc, x_words, x_scales, d_words, d_scales
         scale_planes = keep.tile([P, 3 * ENTRIES], U8, name="scale_planes", tag="query_scales", align_bytes=64)
         d_scale = scale_planes[:, 0:ENTRIES]
         x_scale = scale_planes[:, ENTRIES : 2 * ENTRIES]
-        nc.vector.tensor_copy(d_scale.rearrange("p (t m) -> p t m", t=PACK), d_scale_picked[:].rearrange("p (m t) -> p t m", t=PACK))
+        nc.vector.tensor_copy(d_scale.rearrange("p (t a i) -> p a t i", t=PACK, i=16), d_scale_picked[:].rearrange("p (a i t) -> p a t i", t=PACK, i=16))
         w_scale = scale_planes[:, 2 * ENTRIES : 3 * ENTRIES]
         nc.vector.tensor_copy(w_scale.bitcast(I32), w_scale_dealt[:].bitcast(I32))
         nc.vector.tensor_copy(x_scale.bitcast(I32), x_scale_picked[:].bitcast(I32))
@@ -89,22 +89,25 @@ def tile_picked_reluattn_relu_po_kernel(tc, x_words, x_scales, d_words, d_scales
         for h in range(2):
             nc.vector.tensor_copy(d_word_picked[h][:], d_word_table[:].bitcast(U32).indirect(key_list[:, h * HALF // 16 : (h + 1) * HALF // 16]))
         for h in range(2):
-            dealt = d_word[:].rearrange("p (t m) -> p m t", t=PACK)[:, h * HALF // PACK : (h + 1) * HALF // PACK, :]
-            nc.vector.tensor_copy(dealt, d_word_picked[h][:].rearrange("p (m t) -> p m t", t=PACK))
+            dealt = d_word[:].rearrange("p (t a i) -> p a t i", t=PACK, i=4)[:, h * HALF // 16 : (h + 1) * HALF // 16, :, :]
+            nc.vector.tensor_copy(dealt, d_word_picked[h][:].rearrange("p (a i t) -> p a t i", t=PACK, i=4))
 
         factor = keep.tile([P, ENTRIES], F32, name="factor", tag="key_words", align_bytes=64)
         nc.sync.dma_start(factor[:], cnt)
 
-        x_word = [keep.tile([P, CHUNK], U32, name="x_word%d" % h, align_bytes=64) for h in range(CHUNKS)]
+        pieces = [(0, CHUNK), (CHUNK, CHUNK), (HALF, HALF)]
+        picked = [keep.tile([P, width], U32, name="x_word%d" % first, align_bytes=64) for first, width in pieces]
+        x_word = [picked[0][:], picked[1][:], picked[2][:, 0:CHUNK], picked[2][:, CHUNK:HALF]]
 
         def gather_queries(h):
-            piece = query_list[:, h * CHUNK // 16 : (h + 1) * CHUNK // 16]
-            nc.vector.tensor_copy(x_word[h][:], x_word_table[:].bitcast(U32).indirect(piece))
+            first, width = pieces[h]
+            piece = query_list[:, first // 16 : (first + width) // 16]
+            nc.vector.tensor_copy(picked[h][:], x_word_table[:].bitcast(U32).indirect(piece))
 
         w_word = keep.tile([P, 2 * ENTRIES], U8, name="w_word", align_bytes=64)
 
         def deal_weights():
-            nc.vector.tensor_copy(w_word[:].bitcast(U16).rearrange("p (t m) -> p t m", t=PACK), w_word_raw[:].bitcast(U16).rearrange("p (m t) -> p t m", t=PACK))
+            nc.vector.tensor_copy(w_word[:].bitcast(U16).rearrange("p (t a i) -> p a t i", t=PACK, i=8), w_word_raw[:].bitcast(U16).rearrange("p (a i t) -> p a t i", t=PACK, i=8))
 
         z_word = [keep.tile([P, CHUNK], U32, name="z_word%d" % c, align_bytes=64) for c in range(CHUNKS)]
         z_scale = [keep.tile([P, CHUNK], U8, name="z_scale%d" % c, align_bytes=64) for c in range(CHUNKS)]
@@ -128,7 +131,7 @@ def tile_picked_reluattn_relu_po_kernel(tc, x_words, x_scales, d_words, d_scales
                     out=s[:, t, :],
                     lhsT=d_word[:, t * P : (t + 1) * P].bitcast(FP8X4),
                     lhsT_scale=d_scale[:, t * P : (t + 1) * P],
-                    rhs=x_word[c][:].bitcast(FP8X4),
+                    rhs=x_word[c].bitcast(FP8X4),
                     rhs_scale=x_scale[:, c * CHUNK : (c + 1) * CHUNK],
                     start=True,
                     stop=True,
@@ -201,7 +204,8 @@ def tile_picked_reluattn_relu_po_kernel(tc, x_words, x_scales, d_words, d_scales
                 nc.sync.dma_start(out_words[:, 4 * first : 4 * (first + HALF)].bitcast(I32), y_word[:, first : first + HALF].bitcast(I32))
 
         for c in range(CHUNKS):
-            gather_queries(c)
+            if c < len(pieces):
+                gather_queries(c)
             scores(c)
         deal_weights()
         factor_on_scalar(0)

@@ -18,9 +18,15 @@ P = 128
 PACK = 4
 TABLE = 2048
 ENTRIES = 512
+GROUP = 16
+BLOCK_ROWS = 8
+QUADRANT = 32
+LINE = 16
 CHUNK = 128
 CHUNKS = ENTRIES // CHUNK
-HALF = 256
+LAST = CHUNKS - 1
+HALF = ENTRIES // 2
+QUERY_PIECES = [(0, CHUNK), (CHUNK, CHUNK), (HALF, HALF)]
 SCORE_SCALE = 0.0625
 FLOPS = 2 * 2 * 512 * 512 * 512
 
@@ -32,26 +38,34 @@ def tile_picked_reluattn_relu_po_kernel(tc, x_words, x_scales, d_words, d_scales
         keep = ctx.enter_context(tc.tile_pool(name="keep", bufs=1))
         psum = ctx.enter_context(tc.psum_pool(name="psum", bufs=1))
 
-        key_list = lists.tile([P, ENTRIES // 16], U16, name="key_list")
-        query_list = lists.tile([P, ENTRIES // 16], U16, name="query_list")
+        def slots_of(dealt, run):
+            return dealt.rearrange("p (t a i) -> p a t i", t=PACK, i=run)
+
+        def columns_of(plain, run):
+            return plain.rearrange("p (a i t) -> p a t i", t=PACK, i=run)
+
+        def entries(offsets, first, count):
+            return offsets[:, first // GROUP : (first + count) // GROUP]
+
+        key_list = lists.tile([P, ENTRIES // GROUP], U16, name="key_list")
+        query_list = lists.tile([P, ENTRIES // GROUP], U16, name="query_list")
         d_scale_table = keep.tile([P, TABLE], U8, name="d_scale_table", align_bytes=64)
         w_scale_raw = keep.tile([P, ENTRIES], U8, name="w_scale_raw", align_bytes=64)
-        x_scale_table = keep.tile([P, TABLE], U8, name="x_scale_table", tag="query_scales", align_bytes=64)
+        x_scale_table = keep.tile([P, TABLE], U8, name="x_scale_table", tag="planes", align_bytes=64)
         d_word_table = keep.tile([P, TABLE], I32, name="d_word_table", align_bytes=64)
-        x_word_table = keep.tile([P, TABLE], I32, name="x_word_table", tag="key_words", align_bytes=64)
+        x_word_table = keep.tile([P, TABLE], I32, name="x_word_table", tag="factor", align_bytes=64)
         w_word_raw = keep.tile([P, 2 * ENTRIES], U8, name="w_word_raw", align_bytes=64)
         gain = keep.tile([P, PACK], F32, name="gain", align_bytes=64)
 
-        d_word_rows = d_words[0].rearrange("p n t -> p (n t)").bitcast(I32)
         nc.vector.memset(d_scale_table[:].bitcast(I32), 0)
         nc.vector.memset(x_scale_table[:].bitcast(I32), 0)
-        nc.scalar.dma_start(w_scale_raw[:].bitcast(I32), w1_scales[0].bitcast(I32).unsqueeze(1).broadcast_to([16, 8, ENTRIES // 4]))
+        nc.scalar.dma_start(w_scale_raw[:].bitcast(I32), w1_scales[0].bitcast(I32).unsqueeze(1).broadcast_to([P // BLOCK_ROWS, BLOCK_ROWS, ENTRIES // 4]))
         nc.scalar.dma_start(gain[:], gn.rearrange("(p t) o -> p (t o)", t=PACK))
         nc.sync.dma_start(key_list[:], kidx)
         nc.sync.dma_start(query_list[:], offs)
-        nc.sync.dma_start(d_scale_table[0:P:8, :].bitcast(I32), d_scales[0].bitcast(I32))
-        nc.sync.dma_start(x_scale_table[0:P:8, :].bitcast(I32), x_scales[0].bitcast(I32))
-        nc.sync.dma_start(d_word_table[:], d_word_rows)
+        nc.sync.dma_start(d_scale_table[0:P:BLOCK_ROWS, :].bitcast(I32), d_scales[0].bitcast(I32))
+        nc.sync.dma_start(x_scale_table[0:P:BLOCK_ROWS, :].bitcast(I32), x_scales[0].bitcast(I32))
+        nc.sync.dma_start(d_word_table[:], d_words[0].rearrange("p n t -> p (n t)").bitcast(I32))
         nc.sync.dma_start(x_word_table[:], x_words[0].rearrange("p n t -> p (n t)").bitcast(I32))
         nc.sync.dma_start(w_word_raw[:].bitcast(I32), w1_words[0].bitcast(I32))
 
@@ -60,24 +74,21 @@ def tile_picked_reluattn_relu_po_kernel(tc, x_words, x_scales, d_words, d_scales
         nc.scalar.activation(gain_size[:], gain[:], ACT.Abs, scale=SCORE_SCALE * SCORE_SCALE)
         nc.scalar.activation(gain_root[:], gain_size[:], ACT.Sqrt)
 
-        def move_rows(plane):
-            for b in range(1, 4):
-                nc.scalar.dma_start(plane[b:P:32, :].bitcast(I32), plane[8 * b : P : 32, :].bitcast(I32))
-
         d_scale_picked = keep.tile([P, ENTRIES], U8, name="d_scale_picked", align_bytes=64)
         x_scale_picked = keep.tile([P, ENTRIES], U8, name="x_scale_picked", tag="gain_scaled", align_bytes=64)
         w_scale_dealt = keep.tile([P, ENTRIES], U8, name="w_scale_dealt", align_bytes=64)
         nc.vector.tensor_copy(w_scale_dealt[:].rearrange("p (t m) -> p t m", t=PACK), w_scale_raw[:].rearrange("p (m t) -> p t m", t=PACK))
         nc.vector.tensor_copy(d_scale_picked[:], d_scale_table[:].indirect(key_list[:]))
         nc.vector.tensor_copy(x_scale_picked[:], x_scale_table[:].indirect(query_list[:]))
-        scale_planes = keep.tile([P, 3 * ENTRIES], U8, name="scale_planes", tag="query_scales", align_bytes=64)
+        scale_planes = keep.tile([P, 3 * ENTRIES], U8, name="scale_planes", tag="planes", align_bytes=64)
         d_scale = scale_planes[:, 0:ENTRIES]
         x_scale = scale_planes[:, ENTRIES : 2 * ENTRIES]
-        nc.vector.tensor_copy(d_scale.rearrange("p (t a i) -> p a t i", t=PACK, i=16), d_scale_picked[:].rearrange("p (a i t) -> p a t i", t=PACK, i=16))
         w_scale = scale_planes[:, 2 * ENTRIES : 3 * ENTRIES]
+        nc.vector.tensor_copy(slots_of(d_scale, LINE), columns_of(d_scale_picked[:], LINE))
         nc.vector.tensor_copy(w_scale.bitcast(I32), w_scale_dealt[:].bitcast(I32))
         nc.vector.tensor_copy(x_scale.bitcast(I32), x_scale_picked[:].bitcast(I32))
-        move_rows(scale_planes)
+        for b in range(1, QUADRANT // BLOCK_ROWS):
+            nc.scalar.dma_start(scale_planes[b:P:QUADRANT, :].bitcast(I32), scale_planes[BLOCK_ROWS * b : P : QUADRANT, :].bitcast(I32))
 
         gain_scaled = keep.tile([P, PACK], F32, name="gain_scaled", tag="gain_scaled", align_bytes=64)
         gain_sign = keep.tile([P, CHUNK, PACK], BF16, name="gain_sign", align_bytes=64)
@@ -86,29 +97,17 @@ def tile_picked_reluattn_relu_po_kernel(tc, x_words, x_scales, d_words, d_scales
 
         d_word_picked = [keep.tile([P, HALF], U32, name="d_word_picked%d" % h, align_bytes=64) for h in range(2)]
         d_word = keep.tile([P, ENTRIES], U32, name="d_word", align_bytes=64)
+        words_in_line = LINE // 4
+        lines_in_half = HALF // PACK // words_in_line
         for h in range(2):
-            nc.vector.tensor_copy(d_word_picked[h][:], d_word_table[:].bitcast(U32).indirect(key_list[:, h * HALF // 16 : (h + 1) * HALF // 16]))
+            nc.vector.tensor_copy(d_word_picked[h][:], d_word_table[:].bitcast(U32).indirect(entries(key_list, h * HALF, HALF)))
         for h in range(2):
-            dealt = d_word[:].rearrange("p (t a i) -> p a t i", t=PACK, i=4)[:, h * HALF // 16 : (h + 1) * HALF // 16, :, :]
-            nc.vector.tensor_copy(dealt, d_word_picked[h][:].rearrange("p (a i t) -> p a t i", t=PACK, i=4))
+            nc.vector.tensor_copy(slots_of(d_word[:], words_in_line)[:, h * lines_in_half : (h + 1) * lines_in_half, :, :], columns_of(d_word_picked[h][:], words_in_line))
 
-        factor = keep.tile([P, ENTRIES], F32, name="factor", tag="key_words", align_bytes=64)
-        nc.sync.dma_start(factor[:], cnt)
-
-        pieces = [(0, CHUNK), (CHUNK, CHUNK), (HALF, HALF)]
-        picked = [keep.tile([P, width], U32, name="x_word%d" % first, align_bytes=64) for first, width in pieces]
-        x_word = [picked[0][:], picked[1][:], picked[2][:, 0:CHUNK], picked[2][:, CHUNK:HALF]]
-
-        def gather_queries(h):
-            first, width = pieces[h]
-            piece = query_list[:, first // 16 : (first + width) // 16]
-            nc.vector.tensor_copy(picked[h][:], x_word_table[:].bitcast(U32).indirect(piece))
-
+        factor = keep.tile([P, ENTRIES], F32, name="factor", tag="factor", align_bytes=64)
+        x_word_picked = [keep.tile([P, count], U32, name="x_word%d" % first, align_bytes=64) for first, count in QUERY_PIECES]
+        x_word = [x_word_picked[0][:], x_word_picked[1][:], x_word_picked[2][:, 0:CHUNK], x_word_picked[2][:, CHUNK:HALF]]
         w_word = keep.tile([P, 2 * ENTRIES], U8, name="w_word", align_bytes=64)
-
-        def deal_weights():
-            nc.vector.tensor_copy(w_word[:].bitcast(U16).rearrange("p (t a i) -> p a t i", t=PACK, i=8), w_word_raw[:].bitcast(U16).rearrange("p (a i t) -> p a t i", t=PACK, i=8))
-
         z_word = [keep.tile([P, CHUNK], U32, name="z_word%d" % c, align_bytes=64) for c in range(CHUNKS)]
         z_scale = [keep.tile([P, CHUNK], U8, name="z_scale%d" % c, align_bytes=64) for c in range(CHUNKS)]
         y_word = keep.tile([P, ENTRIES], U32, name="y_word", align_bytes=64)
@@ -116,59 +115,62 @@ def tile_picked_reluattn_relu_po_kernel(tc, x_words, x_scales, d_words, d_scales
         out_rows = out_0.rearrange("(p t) j -> p t j", t=PACK)
         out_words = out_1[0].rearrange("p n t -> p (n t)")
 
-        s_bank, u_tile, z_tile, acc_bank, y_tile, yb_tile = {}, {}, {}, {}, {}, {}
+        score_bank, cofactor, z_tile, sum_bank, y_tile, y_woven = {}, {}, {}, {}, {}, {}
 
-        def in_fours(woven):
+        def queries(c):
+            return slice(c * CHUNK, (c + 1) * CHUNK)
+
+        def woven_side(woven):
             return woven.rearrange("p (a i) t -> p a t i", i=4)
 
-        def from_fours(slots):
+        def slot_side(slots):
             return slots.rearrange("p t (a i) -> p a t i", i=4)
 
+        def gather_queries(piece):
+            first, count = QUERY_PIECES[piece]
+            nc.vector.tensor_copy(x_word_picked[piece][:], x_word_table[:].bitcast(U32).indirect(entries(query_list, first, count)))
+
         def scores(c):
-            s = psum.tile([P, PACK, CHUNK], F32, name="s%d" % c)
+            s = psum.tile([P, PACK, CHUNK], F32, name="score%d" % c)
             for t in range(PACK):
                 nc.tensor.matmul_mx(
                     out=s[:, t, :],
                     lhsT=d_word[:, t * P : (t + 1) * P].bitcast(FP8X4),
                     lhsT_scale=d_scale[:, t * P : (t + 1) * P],
                     rhs=x_word[c].bitcast(FP8X4),
-                    rhs_scale=x_scale[:, c * CHUNK : (c + 1) * CHUNK],
+                    rhs_scale=x_scale[:, queries(c)],
                     start=True,
                     stop=True,
                 )
-            s_bank[c] = s
+            score_bank[c] = s
 
-        def halves(c, split):
-            return [slice(0, CHUNK // 2), slice(CHUNK // 2, CHUNK)] if split else [slice(0, CHUNK)]
-
-        def factor_on_scalar(c):
+        def weigh(c):
             u = keep.tile([P, PACK, CHUNK], F32, name="u%d" % c)
             for t in range(PACK):
-                nc.scalar.activation(u[:, t, :], s_bank[c][:, t, :], ACT.Copy, scale=gain_scaled[:, t : t + 1])
-            u_tile[c] = u[:].rearrange("p t j -> p j t")
+                nc.scalar.activation(u[:, t, :], score_bank[c][:, t, :], ACT.Copy, scale=gain_scaled[:, t : t + 1])
+            cofactor[c] = u
 
-        def product(c):
+        def z_from_scores(c):
             z = keep.tile([P, CHUNK, PACK], BF16, name="z%d" % c, align_bytes=64)
-            for part in halves(c, False):
-                nc.vector.scalar_tensor_tensor(z[:, part, :], s_bank[c][:].rearrange("p t j -> p j t")[:, part, :], 0.0, u_tile[c][:, part, :], MAX, MULT)
+            nc.vector.scalar_tensor_tensor(z[:], score_bank[c][:].rearrange("p t j -> p j t"), 0.0, cofactor[c][:].rearrange("p t j -> p j t"), MAX, MULT)
             z_tile[c] = z
 
-        def size_on_scalar(c):
-            r = keep.tile([P, PACK, CHUNK], F32, name="r%d" % c, tag="r%d" % c, align_bytes=64)
+        def square(c):
+            r = keep.tile([P, PACK, CHUNK], F32, name="relu", tag="relu", align_bytes=64)
             for t in range(PACK):
-                nc.scalar.activation(r[:, t, :], s_bank[c][:, t, :], ACT.Relu, scale=gain_root[:, t : t + 1])
-            u = keep.tile([P, CHUNK, PACK], BF16, name="u%d" % c, align_bytes=64)
-            nc.scalar.activation(in_fours(u[:]), from_fours(r[:]), ACT.Square)
-            u_tile[c] = u[:]
+                nc.scalar.activation(r[:, t, :], score_bank[c][:, t, :], ACT.Relu, scale=gain_root[:, t : t + 1])
+            size = keep.tile([P, CHUNK, PACK], BF16, name="size", align_bytes=64)
+            nc.scalar.activation(woven_side(size[:]), slot_side(r[:]), ACT.Square)
+            cofactor[c] = size
 
-        def signed(c):
+        def z_from_size(c):
             z = keep.tile([P, CHUNK, PACK], BF16, name="z%d" % c, align_bytes=64)
-            nc.vector.tensor_tensor(z[:], u_tile[c], gain_sign[:], MULT)
+            nc.vector.tensor_tensor(z[:], cofactor[c][:], gain_sign[:], MULT)
             z_tile[c] = z
 
         def values(c):
             nc.vector.quantize_mx(out=z_word[c][:].bitcast(FP8X4), scales=z_scale[c][:], in_=z_tile[c][:].rearrange("p j t -> p (j t)"))
-            acc = psum.tile([P, PACK, CHUNK], F32, name="acc%d" % c, tag="acc%d" % c)
+            acc = psum.tile([P, PACK, CHUNK], F32, name="sum%d" % c)
             for t in range(PACK):
                 nc.tensor.matmul_mx(
                     out=acc[:, t, :],
@@ -179,59 +181,56 @@ def tile_picked_reluattn_relu_po_kernel(tc, x_words, x_scales, d_words, d_scales
                     start=True,
                     stop=True,
                 )
-            acc_bank[c] = acc
+            sum_bank[c] = acc
 
         def result(c):
-            cols = slice(c * CHUNK, (c + 1) * CHUNK)
             y = keep.tile([P, PACK, CHUNK], F32, name="y%d" % c)
-            for part in halves(c, c == CHUNKS - 1):
-                width = part.stop - part.start
-                nc.vector.tensor_tensor(y[:, :, part], acc_bank[c][:, :, part], factor[:, cols][:, part].unsqueeze(1).broadcast_to([P, PACK, width]), MULT)
-            nc.sync.dma_start(out_rows[:, :, cols], y[:])
+            nc.vector.tensor_tensor(y[:], sum_bank[c][:], factor[:, queries(c)].unsqueeze(1).broadcast_to([P, PACK, CHUNK]), MULT)
+            nc.sync.dma_start(out_rows[:, :, queries(c)], y[:])
             y_tile[c] = y
 
         def weave(c, copy):
-            yb = keep.tile([P, CHUNK, PACK], BF16, name="yb%d" % c, tag="r%d" % (CHUNKS - 1 - c), align_bytes=64)
-            for part in halves(c, c == CHUNKS - 1):
-                copy(in_fours(yb[:, part, :]), from_fours(y_tile[c][:, :, part]))
-            yb_tile[c] = yb
+            woven = keep.tile([P, CHUNK, PACK], BF16, name="y_woven%d" % c, tag="relu" if c == 0 else "y_woven%d" % c, align_bytes=64)
+            copy(woven_side(woven[:]), slot_side(y_tile[c][:]))
+            y_woven[c] = woven
 
-        def planes(c):
-            cols = slice(c * CHUNK, (c + 1) * CHUNK)
-            nc.vector.quantize_mx(out=y_word[:, cols].bitcast(FP8X4), scales=y_scale[:, cols], in_=yb_tile[c][:].rearrange("p j t -> p (j t)"))
+        def result_planes(c):
+            nc.vector.quantize_mx(out=y_word[:, queries(c)].bitcast(FP8X4), scales=y_scale[:, queries(c)], in_=y_woven[c][:].rearrange("p j t -> p (j t)"))
             if c % 2 == 1:
                 first = (c - 1) * CHUNK
-                nc.sync.dma_start(out_words[:, 4 * first : 4 * (first + HALF)].bitcast(I32), y_word[:, first : first + HALF].bitcast(I32))
+                nc.sync.dma_start(out_words[:, PACK * first : PACK * (first + HALF)].bitcast(I32), y_word[:, first : first + HALF].bitcast(I32))
 
         for c in range(CHUNKS):
-            if c < len(pieces):
+            if c < len(QUERY_PIECES):
                 gather_queries(c)
             scores(c)
-        deal_weights()
-        factor_on_scalar(0)
-        factor_on_scalar(1)
-        factor_on_scalar(2)
-        size_on_scalar(3)
-        product(0)
-        product(1)
+        nc.sync.dma_start(factor[:], cnt)
+        nc.vector.tensor_copy(slots_of(w_word[:].bitcast(U16), LINE // 2), columns_of(w_word_raw[:].bitcast(U16), LINE // 2))
+
+        for c in range(LAST):
+            weigh(c)
+        square(LAST)
+
+        z_from_scores(0)
+        z_from_scores(1)
         values(0)
-        product(2)
+        z_from_scores(2)
         values(1)
         result(0)
-        signed(3)
+        z_from_size(LAST)
         values(2)
-        values(3)
+        values(LAST)
         result(1)
         result(2)
-        weave(0, nc.scalar.copy)
-        weave(1, nc.scalar.copy)
-        weave(2, nc.scalar.copy)
-        planes(0)
-        result(3)
-        planes(1)
-        weave(3, nc.vector.tensor_copy)
-        planes(2)
-        planes(3)
-        for q in range(4):
+        for c in range(LAST):
+            weave(c, nc.scalar.copy)
+        result_planes(0)
+        result(LAST)
+        result_planes(1)
+        weave(LAST, nc.vector.tensor_copy)
+        result_planes(2)
+        result_planes(LAST)
+
+        for q in range(P // QUADRANT):
             queue = nc.scalar if q % 2 == 0 else nc.sync
-            queue.dma_start(out_2[0][4 * q : 4 * q + 4, :].bitcast(I32), y_scale[32 * q : 32 * q + 4, :].bitcast(I32))
+            queue.dma_start(out_2[0][PACK * q : PACK * (q + 1), :].bitcast(I32), y_scale[QUADRANT * q : QUADRANT * q + PACK, :].bitcast(I32))

@@ -150,6 +150,17 @@ def tile_picked_reluattn_relu_po_kernel(tc, x_words, x_scales, d_words, d_scales
                 nc.scalar.activation(u[:, t, :], score_bank[c][:, t, :], ACT.Copy, scale=gain_scaled[:, t : t + 1])
             cofactor[c] = u
 
+        def z_on_vector(c):
+            u = keep.tile([P, CHUNK, PACK], F32, name="u%d" % c)
+            z = keep.tile([P, CHUNK, PACK], BF16, name="z%d" % c, align_bytes=64)
+            s = score_bank[c][:].rearrange("p t j -> p j t")
+            parts = [slice(0, CHUNK // 2), slice(CHUNK // 2, CHUNK)]
+            for part in parts:
+                nc.vector.tensor_tensor(u[:, part, :], s[:, part, :], gain_scaled[:].unsqueeze(1).broadcast_to([P, CHUNK // 2, PACK]), MULT)
+            for part in parts:
+                nc.vector.scalar_tensor_tensor(z[:, part, :], s[:, part, :], 0.0, u[:, part, :], MAX, MULT)
+            z_tile[c] = z
+
         def z_from_scores(c):
             z = keep.tile([P, CHUNK, PACK], BF16, name="z%d" % c, align_bytes=64)
             nc.vector.scalar_tensor_tensor(z[:], score_bank[c][:].rearrange("p t j -> p j t"), 0.0, cofactor[c][:].rearrange("p t j -> p j t"), MAX, MULT)
@@ -205,13 +216,13 @@ def tile_picked_reluattn_relu_po_kernel(tc, x_words, x_scales, d_words, d_scales
                 gather_queries(c)
             scores(c)
         nc.sync.dma_start(factor[:], cnt)
-        nc.vector.tensor_copy(slots_of(w_word[:].bitcast(U16), LINE // 2), columns_of(w_word_raw[:].bitcast(U16), LINE // 2))
+        nc.scalar.copy(slots_of(w_word[:].bitcast(U16), LINE // 2), columns_of(w_word_raw[:].bitcast(U16), LINE // 2))
 
-        for c in range(LAST):
+        for c in range(1, LAST):
             weigh(c)
         square(LAST)
 
-        z_from_scores(0)
+        z_on_vector(0)
         z_from_scores(1)
         values(0)
         z_from_scores(2)

@@ -52,8 +52,8 @@ def tile_picked_reluattn_relu_po_kernel(tc, x_words, x_scales, d_words, d_scales
         d_scale_table = keep.tile([P, TABLE], U8, name="d_scale_table", align_bytes=64)
         w_scale_raw = keep.tile([P, ENTRIES], U8, name="w_scale_raw", align_bytes=64)
         x_scale_table = keep.tile([P, TABLE], U8, name="x_scale_table", tag="planes", align_bytes=64)
-        d_word_table = keep.tile([P, TABLE], I32, name="d_word_table", align_bytes=64)
-        x_word_table = keep.tile([P, TABLE], I32, name="x_word_table", tag="factor", align_bytes=64)
+        d_word_table = keep.tile([P, TABLE], I32, name="d_word_table", tag="factor", align_bytes=64)
+        x_word_table = keep.tile([P, TABLE], I32, name="x_word_table", align_bytes=64)
         w_word_raw = keep.tile([P, 2 * ENTRIES], U8, name="w_word_raw", align_bytes=64)
         gain = keep.tile([P, PACK], F32, name="gain", align_bytes=64)
 
@@ -228,10 +228,10 @@ def tile_picked_reluattn_relu_po_kernel(tc, x_words, x_scales, d_words, d_scales
         z_from_scores(2)
         values(1)
         result(0)
-        z_from_size(LAST)
         values(2)
-        values(LAST)
+        z_from_size(LAST)
         result(1)
+        values(LAST)
         result(2)
         for c in range(LAST):
             weave(c, nc.scalar.copy)

@@ -51,11 +51,11 @@ def tile_picked_reluattn_relu_po_kernel(tc, x_words, x_scales, d_words, d_scales
         query_list = lists.tile([P, ENTRIES // GROUP], U16, name="query_list")
         d_scale_table = keep.tile([P, TABLE], U8, name="d_scale_table", align_bytes=64)
         w_scale_raw = keep.tile([P, ENTRIES], U8, name="w_scale_raw", align_bytes=64)
-        x_scale_table = keep.tile([P, TABLE], U8, name="x_scale_table", tag="planes", align_bytes=64)
+        x_scale_table = keep.tile([P, TABLE], U8, name="x_scale_table", align_bytes=64)
         d_word_table = keep.tile([P, TABLE], I32, name="d_word_table", tag="factor", align_bytes=64)
         x_word_table = keep.tile([P, TABLE], I32, name="x_word_table", align_bytes=64)
         w_word_raw = keep.tile([P, 2 * ENTRIES], U8, name="w_word_raw", align_bytes=64)
-        gain = keep.tile([P, PACK], F32, name="gain", align_bytes=64)
+        gain = keep.tile([P, PACK], F32, name="gain", tag="planes", align_bytes=64)
 
         nc.vector.memset(d_scale_table[:].bitcast(I32), 0)
         nc.vector.memset(x_scale_table[:].bitcast(I32), 0)
@@ -72,10 +72,12 @@ def tile_picked_reluattn_relu_po_kernel(tc, x_words, x_scales, d_words, d_scales
         gain_size = keep.tile([P, PACK], F32, name="gain_size")
         gain_root = keep.tile([P, PACK], F32, name="gain_root")
         nc.scalar.activation(gain_size[:], gain[:], ACT.Abs, scale=SCORE_SCALE * SCORE_SCALE)
+        gain_scaled = keep.tile([P, PACK], F32, name="gain_scaled", align_bytes=64)
+        nc.scalar.activation(gain_scaled[:], gain[:], ACT.Copy, scale=SCORE_SCALE * SCORE_SCALE)
         nc.scalar.activation(gain_root[:], gain_size[:], ACT.Sqrt)
 
         d_scale_picked = keep.tile([P, ENTRIES], U8, name="d_scale_picked", align_bytes=64)
-        x_scale_picked = keep.tile([P, ENTRIES], U8, name="x_scale_picked", tag="gain_scaled", align_bytes=64)
+        x_scale_picked = keep.tile([P, ENTRIES], U8, name="x_scale_picked", tag="gain_sign", align_bytes=64)
         w_scale_dealt = keep.tile([P, ENTRIES], U8, name="w_scale_dealt", align_bytes=64)
         nc.vector.tensor_copy(w_scale_dealt[:].rearrange("p (t m) -> p t m", t=PACK), w_scale_raw[:].rearrange("p (m t) -> p t m", t=PACK))
         nc.vector.tensor_copy(d_scale_picked[:], d_scale_table[:].indirect(key_list[:]))
@@ -90,9 +92,7 @@ def tile_picked_reluattn_relu_po_kernel(tc, x_words, x_scales, d_words, d_scales
         for b in range(1, QUADRANT // BLOCK_ROWS):
             nc.scalar.dma_start(scale_planes[b:P:QUADRANT, :].bitcast(I32), scale_planes[BLOCK_ROWS * b : P : QUADRANT, :].bitcast(I32))
 
-        gain_scaled = keep.tile([P, PACK], F32, name="gain_scaled", tag="gain_scaled", align_bytes=64)
-        gain_sign = keep.tile([P, CHUNK, PACK], BF16, name="gain_sign", align_bytes=64)
-        nc.scalar.activation(gain_scaled[:], gain[:], ACT.Copy, scale=SCORE_SCALE * SCORE_SCALE)
+        gain_sign = keep.tile([P, CHUNK, PACK], BF16, name="gain_sign", tag="gain_sign", align_bytes=64)
         nc.scalar.activation(gain_sign[:], gain_scaled[:].unsqueeze(1).broadcast_to([P, CHUNK, PACK]), ACT.Sign)
 
         d_word_picked = [keep.tile([P, HALF], U32, name="d_word_picked%d" % h, align_bytes=64) for h in range(2)]

@@ -131,7 +131,7 @@ def tile_picked_reluattn_relu_po_kernel(tc, x_words, x_scales, d_words, d_scales
             nc.vector.tensor_copy(x_word_picked[piece][:], x_word_table[:].bitcast(U32).indirect(entries(query_list, first, count)))
 
         def scores(c):
-            s = psum.tile([P, PACK, CHUNK], F32, name="score%d" % c)
+            s = psum.tile([P, PACK, CHUNK], F32, name="score%d" % c, tag="score%d" % c)
             for t in range(PACK):
                 nc.tensor.matmul_mx(
                     out=s[:, t, :],
@@ -181,10 +181,12 @@ def tile_picked_reluattn_relu_po_kernel(tc, x_words, x_scales, d_words, d_scales
 
         def values(c):
             nc.vector.quantize_mx(out=z_word[c][:].bitcast(FP8X4), scales=z_scale[c][:], in_=z_tile[c][:].rearrange("p j t -> p (j t)"))
-            acc = psum.tile([P, PACK, CHUNK], F32, name="sum%d" % c)
+            banks = 2 if c == LAST else 1
+            per_bank = PACK // banks
+            acc = [psum.tile([P, per_bank, CHUNK], F32, name="sum%d_%d" % (c, e), tag="sum%d" % c if e == 0 else "score0") for e in range(banks)]
             for t in range(PACK):
                 nc.tensor.matmul_mx(
-                    out=acc[:, t, :],
+                    out=acc[t // per_bank][:, t % per_bank, :],
                     lhsT=w_word[:, 2 * t * P : 2 * (t + 1) * P].bitcast(FP4X4),
                     lhsT_scale=w_scale[:, t * P : (t + 1) * P],
                     rhs=z_word[c][:].bitcast(FP8X4),
@@ -196,7 +198,9 @@ def tile_picked_reluattn_relu_po_kernel(tc, x_words, x_scales, d_words, d_scales
 
         def result(c):
             y = keep.tile([P, PACK, CHUNK], F32, name="y%d" % c)
-            nc.vector.tensor_tensor(y[:], sum_bank[c][:], factor[:, queries(c)].unsqueeze(1).broadcast_to([P, PACK, CHUNK]), MULT)
+            per_bank = PACK // len(sum_bank[c])
+            for e, acc in enumerate(sum_bank[c]):
+                nc.vector.tensor_tensor(y[:, e * per_bank : (e + 1) * per_bank, :], acc[:], factor[:, queries(c)].unsqueeze(1).broadcast_to([P, per_bank, CHUNK]), MULT)
             nc.sync.dma_start(out_rows[:, :, queries(c)], y[:])
             y_tile[c] = y
 
@@ -235,8 +239,8 @@ def tile_picked_reluattn_relu_po_kernel(tc, x_words, x_scales, d_words, d_scales
         result(2)
         for c in range(LAST):
             weave(c, nc.scalar.copy)
-        result_planes(0)
         result(LAST)
+        result_planes(0)
         result_planes(1)
         weave(LAST, nc.vector.tensor_copy)
         result_planes(2)

@@ -26,6 +26,7 @@ CHUNK = 128
 CHUNKS = ENTRIES // CHUNK
 LAST = CHUNKS - 1
 HALF = ENTRIES // 2
+SCALAR_COLUMNS = 64
 QUERY_PIECES = [(0, CHUNK), (CHUNK, CHUNK), (HALF, HALF)]
 SCORE_SCALE = 0.0625
 FLOPS = 2 * 2 * 512 * 512 * 512
@@ -209,6 +210,12 @@ def tile_picked_reluattn_relu_po_kernel(tc, x_words, x_scales, d_words, d_scales
             copy(woven_side(woven[:]), slot_side(y_tile[c][:]))
             y_woven[c] = woven
 
+        def weave_shared(c):
+            woven = keep.tile([P, CHUNK, PACK], BF16, name="y_woven%d" % c, align_bytes=64)
+            for copy, part in ((nc.scalar.copy, slice(0, SCALAR_COLUMNS)), (nc.vector.tensor_copy, slice(SCALAR_COLUMNS, CHUNK))):
+                copy(woven_side(woven[:, part, :]), slot_side(y_tile[c][:, :, part]))
+            y_woven[c] = woven
+
         def result_planes(c):
             nc.vector.quantize_mx(out=y_word[:, queries(c)].bitcast(FP8X4), scales=y_scale[:, queries(c)], in_=y_woven[c][:].rearrange("p j t -> p (j t)"))
             if c % 2 == 1:
@@ -242,7 +249,7 @@ def tile_picked_reluattn_relu_po_kernel(tc, x_words, x_scales, d_words, d_scales
         result(LAST)
         result_planes(0)
         result_planes(1)
-        weave(LAST, nc.vector.tensor_copy)
+        weave_shared(LAST)
         result_planes(2)
         result_planes(LAST)
 

@@ -29,6 +29,7 @@ HALF = ENTRIES // 2
 SCALAR_COLUMNS = 64
 QUERY_PIECES = [(0, CHUNK), (CHUNK, CHUNK), (HALF, HALF)]
 SCORE_SCALE = 0.0625
+SUM_BANKS = [["sum0"], ["sum1"], ["score0_0"], ["score0_1", "score1_0"]]
 FLOPS = 2 * 2 * 512 * 512 * 512
 
 
@@ -64,21 +65,21 @@ def tile_picked_reluattn_relu_po_kernel(tc, x_words, x_scales, d_words, d_scales
         nc.scalar.dma_start(gain[:], gn.rearrange("(p t) o -> p (t o)", t=PACK))
         nc.sync.dma_start(key_list[:], kidx)
         nc.sync.dma_start(query_list[:], offs)
+        nc.sync.dma_start(w_word_raw[:].bitcast(I32), w1_words[0].bitcast(I32))
         nc.sync.dma_start(d_scale_table[0:P:BLOCK_ROWS, :].bitcast(I32), d_scales[0].bitcast(I32))
         nc.sync.dma_start(x_scale_table[0:P:BLOCK_ROWS, :].bitcast(I32), x_scales[0].bitcast(I32))
         nc.sync.dma_start(d_word_table[:], d_words[0].rearrange("p n t -> p (n t)").bitcast(I32))
         nc.sync.dma_start(x_word_table[:], x_words[0].rearrange("p n t -> p (n t)").bitcast(I32))
-        nc.sync.dma_start(w_word_raw[:].bitcast(I32), w1_words[0].bitcast(I32))
 
         gain_size = keep.tile([P, PACK], F32, name="gain_size")
-        gain_root = keep.tile([P, PACK], F32, name="gain_root")
         nc.scalar.activation(gain_size[:], gain[:], ACT.Abs, scale=SCORE_SCALE * SCORE_SCALE)
         gain_scaled = keep.tile([P, PACK], F32, name="gain_scaled", align_bytes=64)
         nc.scalar.activation(gain_scaled[:], gain[:], ACT.Copy, scale=SCORE_SCALE * SCORE_SCALE)
-        nc.scalar.activation(gain_root[:], gain_size[:], ACT.Sqrt)
+        gain_sign = keep.tile([P, CHUNK, PACK], BF16, name="gain_sign", align_bytes=64)
+        nc.scalar.activation(gain_sign[:], gain_scaled[:].unsqueeze(1).broadcast_to([P, CHUNK, PACK]), ACT.Sign)
 
         d_scale_picked = keep.tile([P, ENTRIES], U8, name="d_scale_picked", align_bytes=64)
-        x_scale_picked = keep.tile([P, ENTRIES], U8, name="x_scale_picked", tag="gain_sign", align_bytes=64)
+        x_scale_picked = keep.tile([P, ENTRIES], U8, name="x_scale_picked", tag="gain_root", align_bytes=64)
         w_scale_dealt = keep.tile([P, ENTRIES], U8, name="w_scale_dealt", align_bytes=64)
         nc.vector.tensor_copy(w_scale_dealt[:].rearrange("p (t m) -> p t m", t=PACK), w_scale_raw[:].rearrange("p (m t) -> p t m", t=PACK))
         nc.vector.tensor_copy(d_scale_picked[:], d_scale_table[:].indirect(key_list[:]))
@@ -93,8 +94,8 @@ def tile_picked_reluattn_relu_po_kernel(tc, x_words, x_scales, d_words, d_scales
         for b in range(1, QUADRANT // BLOCK_ROWS):
             nc.scalar.dma_start(scale_planes[b:P:QUADRANT, :].bitcast(I32), scale_planes[BLOCK_ROWS * b : P : QUADRANT, :].bitcast(I32))
 
-        gain_sign = keep.tile([P, CHUNK, PACK], BF16, name="gain_sign", tag="gain_sign", align_bytes=64)
-        nc.scalar.activation(gain_sign[:], gain_scaled[:].unsqueeze(1).broadcast_to([P, CHUNK, PACK]), ACT.Sign)
+        gain_root = keep.tile([P, PACK], F32, name="gain_root", tag="gain_root", align_bytes=64)
+        nc.scalar.activation(gain_root[:], gain_size[:], ACT.Sqrt)
 
         d_word_picked = [keep.tile([P, HALF], U32, name="d_word_picked%d" % h, align_bytes=64) for h in range(2)]
         d_word = keep.tile([P, ENTRIES], U32, name="d_word", align_bytes=64)
@@ -132,10 +133,12 @@ def tile_picked_reluattn_relu_po_kernel(tc, x_words, x_scales, d_words, d_scales
             nc.vector.tensor_copy(x_word_picked[piece][:], x_word_table[:].bitcast(U32).indirect(entries(query_list, first, count)))
 
         def scores(c):
-            s = psum.tile([P, PACK, CHUNK], F32, name="score%d" % c, tag="score%d" % c)
+            banks = 2 if c < 2 else 1
+            per_bank = PACK // banks
+            s = [psum.tile([P, per_bank, CHUNK], F32, name="score%d_%d" % (c, e), tag="score%d_%d" % (c, e)) for e in range(banks)]
             for t in range(PACK):
                 nc.tensor.matmul_mx(
-                    out=s[:, t, :],
+                    out=s[t // per_bank][:, t % per_bank, :],
                     lhsT=d_word[:, t * P : (t + 1) * P].bitcast(FP8X4),
                     lhsT_scale=d_scale[:, t * P : (t + 1) * P],
                     rhs=x_word[c].bitcast(FP8X4),
@@ -143,13 +146,24 @@ def tile_picked_reluattn_relu_po_kernel(tc, x_words, x_scales, d_words, d_scales
                     start=True,
                     stop=True,
                 )
-            score_bank[c] = s
+            score_bank[c] = s if banks > 1 else s[0]
 
         def weigh(c):
             u = keep.tile([P, PACK, CHUNK], F32, name="u%d" % c)
             for t in range(PACK):
                 nc.scalar.activation(u[:, t, :], score_bank[c][:, t, :], ACT.Copy, scale=gain_scaled[:, t : t + 1])
             cofactor[c] = u
+
+        def weigh_pairs(c):
+            u = [keep.tile([P, 2, CHUNK], F32, name="u%d_%d" % (c, e)) for e in range(2)]
+            for t in range(PACK):
+                nc.scalar.activation(u[t // 2][:, t % 2, :], score_bank[c][t // 2][:, t % 2, :], ACT.Copy, scale=gain_scaled[:, t : t + 1])
+            cofactor[c] = u
+
+        def z_pair(c, e):
+            if e == 0:
+                z_tile[c] = keep.tile([P, CHUNK, PACK], BF16, name="z%d" % c, align_bytes=64)
+            nc.vector.scalar_tensor_tensor(z_tile[c][:, :, 2 * e : 2 * e + 2], score_bank[c][e][:].rearrange("p t j -> p j t"), 0.0, cofactor[c][e][:].rearrange("p t j -> p j t"), MAX, MULT)
 
         def z_on_vector(c):
             u = keep.tile([P, CHUNK, PACK], F32, name="u%d" % c)
@@ -184,7 +198,7 @@ def tile_picked_reluattn_relu_po_kernel(tc, x_words, x_scales, d_words, d_scales
             nc.vector.quantize_mx(out=z_word[c][:].bitcast(FP8X4), scales=z_scale[c][:], in_=z_tile[c][:].rearrange("p j t -> p (j t)"))
             banks = 2 if c == LAST else 1
             per_bank = PACK // banks
-            acc = [psum.tile([P, per_bank, CHUNK], F32, name="sum%d_%d" % (c, e), tag="sum%d" % c if e == 0 else "score0") for e in range(banks)]
+            acc = [psum.tile([P, per_bank, CHUNK], F32, name="sum%d_%d" % (c, e), tag=SUM_BANKS[c][e]) for e in range(banks)]
             for t in range(PACK):
                 nc.tensor.matmul_mx(
                     out=acc[t // per_bank][:, t % per_bank, :],
@@ -229,13 +243,16 @@ def tile_picked_reluattn_relu_po_kernel(tc, x_words, x_scales, d_words, d_scales
         nc.sync.dma_start(factor[:], cnt)
         nc.scalar.copy(slots_of(w_word[:].bitcast(U16), LINE // 2), columns_of(w_word_raw[:].bitcast(U16), LINE // 2))
 
-        for c in range(1, LAST):
-            weigh(c)
+        weigh_pairs(0)
+        weigh_pairs(1)
+        weigh(2)
         square(LAST)
 
-        z_on_vector(0)
-        z_from_scores(1)
+        z_pair(0, 0)
+        z_pair(0, 1)
+        z_pair(1, 0)
         values(0)
+        z_pair(1, 1)
         z_from_scores(2)
         values(1)
         result(0)

@@ -22,6 +22,7 @@ GROUP = 16
 BLOCK_ROWS = 8
 QUADRANT = 32
 LINE = 16
+DMA_ALIGN = 256
 CHUNK = 128
 CHUNKS = ENTRIES // CHUNK
 LAST = CHUNKS - 1
@@ -29,6 +30,7 @@ HALF = ENTRIES // 2
 SCALAR_COLUMNS = 64
 QUERY_PIECES = [(0, CHUNK), (CHUNK, CHUNK), (HALF, HALF)]
 SCORE_SCALE = 0.0625
+SCORE_BANKS = [2, 2, 1, 1]
 SUM_BANKS = [["sum0"], ["sum1"], ["score0_0"], ["score0_1", "score1_0"]]
 FLOPS = 2 * 2 * 512 * 512 * 512
 
@@ -51,13 +53,13 @@ def tile_picked_reluattn_relu_po_kernel(tc, x_words, x_scales, d_words, d_scales
 
         key_list = lists.tile([P, ENTRIES // GROUP], U16, name="key_list")
         query_list = lists.tile([P, ENTRIES // GROUP], U16, name="query_list")
-        d_scale_table = keep.tile([P, TABLE], U8, name="d_scale_table", align_bytes=64)
-        w_scale_raw = keep.tile([P, ENTRIES], U8, name="w_scale_raw", align_bytes=64)
-        x_scale_table = keep.tile([P, TABLE], U8, name="x_scale_table", align_bytes=64)
-        d_word_table = keep.tile([P, TABLE], I32, name="d_word_table", tag="factor", align_bytes=64)
-        x_word_table = keep.tile([P, TABLE], I32, name="x_word_table", align_bytes=64)
-        w_word_raw = keep.tile([P, 2 * ENTRIES], U8, name="w_word_raw", align_bytes=64)
-        gain = keep.tile([P, PACK], F32, name="gain", tag="planes", align_bytes=64)
+        d_scale_table = keep.tile([P, TABLE], U8, name="d_scale_table", align_bytes=DMA_ALIGN)
+        w_scale_raw = keep.tile([P, ENTRIES], U8, name="w_scale_raw", align_bytes=DMA_ALIGN)
+        x_scale_table = keep.tile([P, TABLE], U8, name="x_scale_table", align_bytes=DMA_ALIGN)
+        d_word_table = keep.tile([P, TABLE], I32, name="d_word_table", tag="factor", align_bytes=DMA_ALIGN)
+        x_word_table = keep.tile([P, TABLE], I32, name="x_word_table", align_bytes=DMA_ALIGN)
+        w_word_raw = keep.tile([P, 2 * ENTRIES], U8, name="w_word_raw", align_bytes=DMA_ALIGN)
+        gain = keep.tile([P, PACK], F32, name="gain", tag="planes", align_bytes=DMA_ALIGN)
 
         nc.vector.memset(d_scale_table[:].bitcast(I32), 0)
         nc.vector.memset(x_scale_table[:].bitcast(I32), 0)
@@ -84,7 +86,7 @@ def tile_picked_reluattn_relu_po_kernel(tc, x_words, x_scales, d_words, d_scales
         nc.vector.tensor_copy(w_scale_dealt[:].rearrange("p (t m) -> p t m", t=PACK), w_scale_raw[:].rearrange("p (m t) -> p t m", t=PACK))
         nc.vector.tensor_copy(d_scale_picked[:], d_scale_table[:].indirect(key_list[:]))
         nc.vector.tensor_copy(x_scale_picked[:], x_scale_table[:].indirect(query_list[:]))
-        scale_planes = keep.tile([P, 3 * ENTRIES], U8, name="scale_planes", tag="planes", align_bytes=64)
+        scale_planes = keep.tile([P, 3 * ENTRIES], U8, name="scale_planes", tag="planes", align_bytes=DMA_ALIGN)
         d_scale = scale_planes[:, 0:ENTRIES]
         x_scale = scale_planes[:, ENTRIES : 2 * ENTRIES]
         w_scale = scale_planes[:, 2 * ENTRIES : 3 * ENTRIES]
@@ -106,14 +108,14 @@ def tile_picked_reluattn_relu_po_kernel(tc, x_words, x_scales, d_words, d_scales
         for h in range(2):
             nc.vector.tensor_copy(slots_of(d_word[:], words_in_line)[:, h * lines_in_half : (h + 1) * lines_in_half, :, :], columns_of(d_word_picked[h][:], words_in_line))
 
-        factor = keep.tile([P, ENTRIES], F32, name="factor", tag="factor", align_bytes=64)
+        factor = keep.tile([P, ENTRIES], F32, name="factor", tag="factor", align_bytes=DMA_ALIGN)
         x_word_picked = [keep.tile([P, count], U32, name="x_word%d" % first, align_bytes=64) for first, count in QUERY_PIECES]
         x_word = [x_word_picked[0][:], x_word_picked[1][:], x_word_picked[2][:, 0:CHUNK], x_word_picked[2][:, CHUNK:HALF]]
         w_word = keep.tile([P, 2 * ENTRIES], U8, name="w_word", align_bytes=64)
         z_word = [keep.tile([P, CHUNK], U32, name="z_word%d" % c, align_bytes=64) for c in range(CHUNKS)]
         z_scale = [keep.tile([P, CHUNK], U8, name="z_scale%d" % c, align_bytes=64) for c in range(CHUNKS)]
-        y_word = keep.tile([P, ENTRIES], U32, name="y_word", align_bytes=64)
-        y_scale = keep.tile([P, ENTRIES], U8, name="y_scale", align_bytes=64)
+        y_word = keep.tile([P, ENTRIES], U32, name="y_word", align_bytes=DMA_ALIGN)
+        y_scale = keep.tile([P, ENTRIES], U8, name="y_scale", align_bytes=DMA_ALIGN)
         out_rows = out_0.rearrange("(p t) j -> p t j", t=PACK)
         out_words = out_1[0].rearrange("p n t -> p (n t)")
 
@@ -133,9 +135,8 @@ def tile_picked_reluattn_relu_po_kernel(tc, x_words, x_scales, d_words, d_scales
             nc.vector.tensor_copy(x_word_picked[piece][:], x_word_table[:].bitcast(U32).indirect(entries(query_list, first, count)))
 
         def scores(c):
-            banks = 2 if c < 2 else 1
-            per_bank = PACK // banks
-            s = [psum.tile([P, per_bank, CHUNK], F32, name="score%d_%d" % (c, e), tag="score%d_%d" % (c, e)) for e in range(banks)]
+            per_bank = PACK // SCORE_BANKS[c]
+            s = [psum.tile([P, per_bank, CHUNK], F32, name="score%d_%d" % (c, e), tag="score%d_%d" % (c, e)) for e in range(SCORE_BANKS[c])]
             for t in range(PACK):
                 nc.tensor.matmul_mx(
                     out=s[t // per_bank][:, t % per_bank, :],
@@ -146,45 +147,26 @@ def tile_picked_reluattn_relu_po_kernel(tc, x_words, x_scales, d_words, d_scales
                     start=True,
                     stop=True,
                 )
-            score_bank[c] = s if banks > 1 else s[0]
+            score_bank[c] = s
 
         def weigh(c):
-            u = keep.tile([P, PACK, CHUNK], F32, name="u%d" % c)
+            per_bank = PACK // SCORE_BANKS[c]
+            u = [keep.tile([P, per_bank, CHUNK], F32, name="u%d_%d" % (c, e)) for e in range(SCORE_BANKS[c])]
             for t in range(PACK):
-                nc.scalar.activation(u[:, t, :], score_bank[c][:, t, :], ACT.Copy, scale=gain_scaled[:, t : t + 1])
+                e, slot = divmod(t, per_bank)
+                nc.scalar.activation(u[e][:, slot, :], score_bank[c][e][:, slot, :], ACT.Copy, scale=gain_scaled[:, t : t + 1])
             cofactor[c] = u
 
-        def weigh_pairs(c):
-            u = [keep.tile([P, 2, CHUNK], F32, name="u%d_%d" % (c, e)) for e in range(2)]
-            for t in range(PACK):
-                nc.scalar.activation(u[t // 2][:, t % 2, :], score_bank[c][t // 2][:, t % 2, :], ACT.Copy, scale=gain_scaled[:, t : t + 1])
-            cofactor[c] = u
-
-        def z_pair(c, e):
+        def z_from_scores(c, e):
+            per_bank = PACK // SCORE_BANKS[c]
             if e == 0:
                 z_tile[c] = keep.tile([P, CHUNK, PACK], BF16, name="z%d" % c, align_bytes=64)
-            nc.vector.scalar_tensor_tensor(z_tile[c][:, :, 2 * e : 2 * e + 2], score_bank[c][e][:].rearrange("p t j -> p j t"), 0.0, cofactor[c][e][:].rearrange("p t j -> p j t"), MAX, MULT)
-
-        def z_on_vector(c):
-            u = keep.tile([P, CHUNK, PACK], F32, name="u%d" % c)
-            z = keep.tile([P, CHUNK, PACK], BF16, name="z%d" % c, align_bytes=64)
-            s = score_bank[c][:].rearrange("p t j -> p j t")
-            parts = [slice(0, CHUNK // 2), slice(CHUNK // 2, CHUNK)]
-            for part in parts:
-                nc.vector.tensor_tensor(u[:, part, :], s[:, part, :], gain_scaled[:].unsqueeze(1).broadcast_to([P, CHUNK // 2, PACK]), MULT)
-            for part in parts:
-                nc.vector.scalar_tensor_tensor(z[:, part, :], s[:, part, :], 0.0, u[:, part, :], MAX, MULT)
-            z_tile[c] = z
-
-        def z_from_scores(c):
-            z = keep.tile([P, CHUNK, PACK], BF16, name="z%d" % c, align_bytes=64)
-            nc.vector.scalar_tensor_tensor(z[:], score_bank[c][:].rearrange("p t j -> p j t"), 0.0, cofactor[c][:].rearrange("p t j -> p j t"), MAX, MULT)
-            z_tile[c] = z
+            nc.vector.scalar_tensor_tensor(z_tile[c][:, :, e * per_bank : (e + 1) * per_bank], score_bank[c][e][:].rearrange("p t j -> p j t"), 0.0, cofactor[c][e][:].rearrange("p t j -> p j t"), MAX, MULT)
 
         def square(c):
             r = keep.tile([P, PACK, CHUNK], F32, name="relu", tag="relu", align_bytes=64)
             for t in range(PACK):
-                nc.scalar.activation(r[:, t, :], score_bank[c][:, t, :], ACT.Relu, scale=gain_root[:, t : t + 1])
+                nc.scalar.activation(r[:, t, :], score_bank[c][0][:, t, :], ACT.Relu, scale=gain_root[:, t : t + 1])
             size = keep.tile([P, CHUNK, PACK], BF16, name="size", align_bytes=64)
             nc.scalar.activation(woven_side(size[:]), slot_side(r[:]), ACT.Square)
             cofactor[c] = size
@@ -196,9 +178,8 @@ def tile_picked_reluattn_relu_po_kernel(tc, x_words, x_scales, d_words, d_scales
 
         def values(c):
             nc.vector.quantize_mx(out=z_word[c][:].bitcast(FP8X4), scales=z_scale[c][:], in_=z_tile[c][:].rearrange("p j t -> p (j t)"))
-            banks = 2 if c == LAST else 1
-            per_bank = PACK // banks
-            acc = [psum.tile([P, per_bank, CHUNK], F32, name="sum%d_%d" % (c, e), tag=SUM_BANKS[c][e]) for e in range(banks)]
+            per_bank = PACK // len(SUM_BANKS[c])
+            acc = [psum.tile([P, per_bank, CHUNK], F32, name="sum%d_%d" % (c, e), tag=bank) for e, bank in enumerate(SUM_BANKS[c])]
             for t in range(PACK):
                 nc.tensor.matmul_mx(
                     out=acc[t // per_bank][:, t % per_bank, :],
@@ -212,7 +193,7 @@ def tile_picked_reluattn_relu_po_kernel(tc, x_words, x_scales, d_words, d_scales
             sum_bank[c] = acc
 
         def result(c):
-            y = keep.tile([P, PACK, CHUNK], F32, name="y%d" % c)
+            y = keep.tile([P, PACK, CHUNK], F32, name="y%d" % c, align_bytes=DMA_ALIGN)
             per_bank = PACK // len(sum_bank[c])
             for e, acc in enumerate(sum_bank[c]):
                 nc.vector.tensor_tensor(y[:, e * per_bank : (e + 1) * per_bank, :], acc[:], factor[:, queries(c)].unsqueeze(1).broadcast_to([P, per_bank, CHUNK]), MULT)
@@ -243,17 +224,16 @@ def tile_picked_reluattn_relu_po_kernel(tc, x_words, x_scales, d_words, d_scales
         nc.sync.dma_start(factor[:], cnt)
         nc.scalar.copy(slots_of(w_word[:].bitcast(U16), LINE // 2), columns_of(w_word_raw[:].bitcast(U16), LINE // 2))
 
-        weigh_pairs(0)
-        weigh_pairs(1)
-        weigh(2)
+        for c in range(LAST):
+            weigh(c)
         square(LAST)
 
-        z_pair(0, 0)
-        z_pair(0, 1)
-        z_pair(1, 0)
+        z_from_scores(0, 0)
+        z_from_scores(0, 1)
+        z_from_scores(1, 0)
         values(0)
-        z_pair(1, 1)
-        z_from_scores(2)
+        z_from_scores(1, 1)
+        z_from_scores(2, 0)
         values(1)
         result(0)
         values(2)

@@ -51,13 +51,13 @@ def tile_picked_reluattn_relu_po_kernel(tc, x_words, x_scales, d_words, d_scales
         def entries(offsets, first, count):
             return offsets[:, first // GROUP : (first + count) // GROUP]
 
-        key_list = lists.tile([P, ENTRIES // GROUP], U16, name="key_list")
-        query_list = lists.tile([P, ENTRIES // GROUP], U16, name="query_list")
+        key_list = lists.tile([P, ENTRIES // GROUP], U16, name="key_list", align_bytes=DMA_ALIGN)
+        query_list = lists.tile([P, ENTRIES // GROUP], U16, name="query_list", align_bytes=DMA_ALIGN)
         d_scale_table = keep.tile([P, TABLE], U8, name="d_scale_table", align_bytes=DMA_ALIGN)
         w_scale_raw = keep.tile([P, ENTRIES], U8, name="w_scale_raw", align_bytes=DMA_ALIGN)
         x_scale_table = keep.tile([P, TABLE], U8, name="x_scale_table", align_bytes=DMA_ALIGN)
-        d_word_table = keep.tile([P, TABLE], I32, name="d_word_table", tag="factor", align_bytes=DMA_ALIGN)
-        x_word_table = keep.tile([P, TABLE], I32, name="x_word_table", align_bytes=DMA_ALIGN)
+        d_word_table = keep.tile([P, TABLE], I32, name="d_word_table", align_bytes=DMA_ALIGN)
+        x_word_table = keep.tile([P, TABLE], I32, name="x_word_table", tag="factor", align_bytes=DMA_ALIGN)
         w_word_raw = keep.tile([P, 2 * ENTRIES], U8, name="w_word_raw", align_bytes=DMA_ALIGN)
         gain = keep.tile([P, PACK], F32, name="gain", tag="planes", align_bytes=DMA_ALIGN)
 
@@ -90,8 +90,8 @@ def tile_picked_reluattn_relu_po_kernel(tc, x_words, x_scales, d_words, d_scales
         d_scale = scale_planes[:, 0:ENTRIES]
         x_scale = scale_planes[:, ENTRIES : 2 * ENTRIES]
         w_scale = scale_planes[:, 2 * ENTRIES : 3 * ENTRIES]
+        nc.scalar.copy(w_scale.bitcast(U32), w_scale_dealt[:].bitcast(U32))
         nc.vector.tensor_copy(slots_of(d_scale, LINE), columns_of(d_scale_picked[:], LINE))
-        nc.vector.tensor_copy(w_scale.bitcast(I32), w_scale_dealt[:].bitcast(I32))
         nc.vector.tensor_copy(x_scale.bitcast(I32), x_scale_picked[:].bitcast(I32))
         for b in range(1, QUADRANT // BLOCK_ROWS):
             nc.scalar.dma_start(scale_planes[b:P:QUADRANT, :].bitcast(I32), scale_planes[BLOCK_ROWS * b : P : QUADRANT, :].bitcast(I32))

from contextlib import ExitStack

import concourse.mybir as mybir

F32 = mybir.dt.float32
BF16 = mybir.dt.bfloat16
I32 = mybir.dt.int32
U32 = mybir.dt.uint32
U16 = mybir.dt.uint16
U8 = mybir.dt.uint8
FP8X4 = mybir.dt.float8_e4m3fn_x4
FP4X4 = mybir.dt.float4_e2m1fn_x4
ACT = mybir.ActivationFunctionType
MULT = mybir.AluOpType.mult
MAX = mybir.AluOpType.max

P = 128
PACK = 4
TABLE = 2048
ENTRIES = 512
GROUP = 16
BLOCK_ROWS = 8
QUADRANT = 32
LINE = 16
DMA_ALIGN = 256
CHUNK = 128
CHUNKS = ENTRIES // CHUNK
LAST = CHUNKS - 1
HALF = ENTRIES // 2
SCALAR_COLUMNS = 64
QUERY_PIECES = [(0, CHUNK), (CHUNK, CHUNK), (HALF, HALF)]
SCORE_SCALE = 0.0625
SCORE_BANKS = [2, 2, 1, 1]
SUM_BANKS = [["sum0"], ["sum1"], ["score0_0"], ["score0_1", "score1_0"]]
FLOPS = 2 * 2 * 512 * 512 * 512


def tile_picked_reluattn_relu_po_kernel(tc, x_words, x_scales, d_words, d_scales, cnt, gn, w1_words, w1_scales, offs, kidx, out_0, out_1, out_2):
    nc = tc.nc
    with ExitStack() as ctx:
        lists = ctx.enter_context(tc.tile_pool(name="lists", bufs=1))
        keep = ctx.enter_context(tc.tile_pool(name="keep", bufs=1))
        psum = ctx.enter_context(tc.psum_pool(name="psum", bufs=1))

        def slots_of(dealt, run):
            return dealt.rearrange("p (t a i) -> p a t i", t=PACK, i=run)

        def columns_of(plain, run):
            return plain.rearrange("p (a i t) -> p a t i", t=PACK, i=run)

        def entries(offsets, first, count):
            return offsets[:, first // GROUP : (first + count) // GROUP]

        key_list = lists.tile([P, ENTRIES // GROUP], U16, name="key_list", align_bytes=DMA_ALIGN)
        query_list = lists.tile([P, ENTRIES // GROUP], U16, name="query_list", align_bytes=DMA_ALIGN)
        d_scale_table = keep.tile([P, TABLE], U8, name="d_scale_table", align_bytes=DMA_ALIGN)
        w_scale_raw = keep.tile([P, ENTRIES], U8, name="w_scale_raw", align_bytes=DMA_ALIGN)
        x_scale_table = keep.tile([P, TABLE], U8, name="x_scale_table", align_bytes=DMA_ALIGN)
        d_word_table = keep.tile([P, TABLE], I32, name="d_word_table", align_bytes=DMA_ALIGN)
        x_word_table = keep.tile([P, TABLE], I32, name="x_word_table", tag="factor", align_bytes=DMA_ALIGN)
        w_word_raw = keep.tile([P, 2 * ENTRIES], U8, name="w_word_raw", align_bytes=DMA_ALIGN)
        gain = keep.tile([P, PACK], F32, name="gain", tag="planes", align_bytes=DMA_ALIGN)

        nc.vector.memset(d_scale_table[:].bitcast(I32), 0)
        nc.vector.memset(x_scale_table[:].bitcast(I32), 0)
        nc.scalar.dma_start(w_scale_raw[:].bitcast(I32), w1_scales[0].bitcast(I32).unsqueeze(1).broadcast_to([P // BLOCK_ROWS, BLOCK_ROWS, ENTRIES // 4]))
        nc.scalar.dma_start(gain[:], gn.rearrange("(p t) o -> p (t o)", t=PACK))
        nc.sync.dma_start(key_list[:], kidx)
        nc.sync.dma_start(query_list[:], offs)
        nc.sync.dma_start(w_word_raw[:].bitcast(I32), w1_words[0].bitcast(I32))
        nc.sync.dma_start(d_scale_table[0:P:BLOCK_ROWS, :].bitcast(I32), d_scales[0].bitcast(I32))
        nc.sync.dma_start(x_scale_table[0:P:BLOCK_ROWS, :].bitcast(I32), x_scales[0].bitcast(I32))
        nc.sync.dma_start(d_word_table[:], d_words[0].rearrange("p n t -> p (n t)").bitcast(I32))
        nc.sync.dma_start(x_word_table[:], x_words[0].rearrange("p n t -> p (n t)").bitcast(I32))

        gain_size = keep.tile([P, PACK], F32, name="gain_size")
        nc.scalar.activation(gain_size[:], gain[:], ACT.Abs, scale=SCORE_SCALE * SCORE_SCALE)
        gain_scaled = keep.tile([P, PACK], F32, name="gain_scaled", align_bytes=64)
        nc.scalar.activation(gain_scaled[:], gain[:], ACT.Copy, scale=SCORE_SCALE * SCORE_SCALE)
        gain_sign = keep.tile([P, CHUNK, PACK], BF16, name="gain_sign", align_bytes=64)
        nc.scalar.activation(gain_sign[:], gain_scaled[:].unsqueeze(1).broadcast_to([P, CHUNK, PACK]), ACT.Sign)

        d_scale_picked = keep.tile([P, ENTRIES], U8, name="d_scale_picked", align_bytes=64)
        x_scale_picked = keep.tile([P, ENTRIES], U8, name="x_scale_picked", tag="gain_root", align_bytes=64)
        w_scale_dealt = keep.tile([P, ENTRIES], U8, name="w_scale_dealt", align_bytes=64)
        nc.vector.tensor_copy(w_scale_dealt[:].rearrange("p (t m) -> p t m", t=PACK), w_scale_raw[:].rearrange("p (m t) -> p t m", t=PACK))
        nc.vector.tensor_copy(d_scale_picked[:], d_scale_table[:].indirect(key_list[:]))
        nc.vector.tensor_copy(x_scale_picked[:], x_scale_table[:].indirect(query_list[:]))
        scale_planes = keep.tile([P, 3 * ENTRIES], U8, name="scale_planes", tag="planes", align_bytes=DMA_ALIGN)
        d_scale = scale_planes[:, 0:ENTRIES]
        x_scale = scale_planes[:, ENTRIES : 2 * ENTRIES]
        w_scale = scale_planes[:, 2 * ENTRIES : 3 * ENTRIES]
        nc.scalar.copy(w_scale.bitcast(U32), w_scale_dealt[:].bitcast(U32))
        nc.vector.tensor_copy(slots_of(d_scale, LINE), columns_of(d_scale_picked[:], LINE))
        nc.vector.tensor_copy(x_scale.bitcast(I32), x_scale_picked[:].bitcast(I32))
        for b in range(1, QUADRANT // BLOCK_ROWS):
            nc.scalar.dma_start(scale_planes[b:P:QUADRANT, :].bitcast(I32), scale_planes[BLOCK_ROWS * b : P : QUADRANT, :].bitcast(I32))

        gain_root = keep.tile([P, PACK], F32, name="gain_root", tag="gain_root", align_bytes=64)
        nc.scalar.activation(gain_root[:], gain_size[:], ACT.Sqrt)

        d_word_picked = [keep.tile([P, HALF], U32, name="d_word_picked%d" % h, align_bytes=64) for h in range(2)]
        d_word = keep.tile([P, ENTRIES], U32, name="d_word", align_bytes=64)
        words_in_line = LINE // 4
        lines_in_half = HALF // PACK // words_in_line
        for h in range(2):
            nc.vector.tensor_copy(d_word_picked[h][:], d_word_table[:].bitcast(U32).indirect(entries(key_list, h * HALF, HALF)))
        for h in range(2):
            nc.vector.tensor_copy(slots_of(d_word[:], words_in_line)[:, h * lines_in_half : (h + 1) * lines_in_half, :, :], columns_of(d_word_picked[h][:], words_in_line))

        factor = keep.tile([P, ENTRIES], F32, name="factor", tag="factor", align_bytes=DMA_ALIGN)
        x_word_picked = [keep.tile([P, count], U32, name="x_word%d" % first, align_bytes=64) for first, count in QUERY_PIECES]
        x_word = [x_word_picked[0][:], x_word_picked[1][:], x_word_picked[2][:, 0:CHUNK], x_word_picked[2][:, CHUNK:HALF]]
        w_word = keep.tile([P, 2 * ENTRIES], U8, name="w_word", align_bytes=64)
        z_word = [keep.tile([P, CHUNK], U32, name="z_word%d" % c, align_bytes=64) for c in range(CHUNKS)]
        z_scale = [keep.tile([P, CHUNK], U8, name="z_scale%d" % c, align_bytes=64) for c in range(CHUNKS)]
        y_word = keep.tile([P, ENTRIES], U32, name="y_word", align_bytes=DMA_ALIGN)
        y_scale = keep.tile([P, ENTRIES], U8, name="y_scale", align_bytes=DMA_ALIGN)
        out_rows = out_0.rearrange("(p t) j -> p t j", t=PACK)
        out_words = out_1[0].rearrange("p n t -> p (n t)")

        score_bank, cofactor, z_tile, sum_bank, y_tile, y_woven = {}, {}, {}, {}, {}, {}

        def queries(c):
            return slice(c * CHUNK, (c + 1) * CHUNK)

        def woven_side(woven):
            return woven.rearrange("p (a i) t -> p a t i", i=4)

        def slot_side(slots):
            return slots.rearrange("p t (a i) -> p a t i", i=4)

        def gather_queries(piece):
            first, count = QUERY_PIECES[piece]
            nc.vector.tensor_copy(x_word_picked[piece][:], x_word_table[:].bitcast(U32).indirect(entries(query_list, first, count)))

        def scores(c):
            per_bank = PACK // SCORE_BANKS[c]
            s = [psum.tile([P, per_bank, CHUNK], F32, name="score%d_%d" % (c, e), tag="score%d_%d" % (c, e)) for e in range(SCORE_BANKS[c])]
            for t in range(PACK):
                nc.tensor.matmul_mx(
                    out=s[t // per_bank][:, t % per_bank, :],
                    lhsT=d_word[:, t * P : (t + 1) * P].bitcast(FP8X4),
                    lhsT_scale=d_scale[:, t * P : (t + 1) * P],
                    rhs=x_word[c].bitcast(FP8X4),
                    rhs_scale=x_scale[:, queries(c)],
                    start=True,
                    stop=True,
                )
            score_bank[c] = s

        def weigh(c):
            per_bank = PACK // SCORE_BANKS[c]
            u = [keep.tile([P, per_bank, CHUNK], F32, name="u%d_%d" % (c, e)) for e in range(SCORE_BANKS[c])]
            for t in range(PACK):
                e, slot = divmod(t, per_bank)
                nc.scalar.activation(u[e][:, slot, :], score_bank[c][e][:, slot, :], ACT.Copy, scale=gain_scaled[:, t : t + 1])
            cofactor[c] = u

        def z_from_scores(c, e):
            per_bank = PACK // SCORE_BANKS[c]
            if e == 0:
                z_tile[c] = keep.tile([P, CHUNK, PACK], BF16, name="z%d" % c, align_bytes=64)
            nc.vector.scalar_tensor_tensor(z_tile[c][:, :, e * per_bank : (e + 1) * per_bank], score_bank[c][e][:].rearrange("p t j -> p j t"), 0.0, cofactor[c][e][:].rearrange("p t j -> p j t"), MAX, MULT)

        def square(c):
            r = keep.tile([P, PACK, CHUNK], F32, name="relu", tag="relu", align_bytes=64)
            for t in range(PACK):
                nc.scalar.activation(r[:, t, :], score_bank[c][0][:, t, :], ACT.Relu, scale=gain_root[:, t : t + 1])
            size = keep.tile([P, CHUNK, PACK], BF16, name="size", align_bytes=64)
            nc.scalar.activation(woven_side(size[:]), slot_side(r[:]), ACT.Square)
            cofactor[c] = size

        def z_from_size(c):
            z = keep.tile([P, CHUNK, PACK], BF16, name="z%d" % c, align_bytes=64)
            nc.vector.tensor_tensor(z[:], cofactor[c][:], gain_sign[:], MULT)
            z_tile[c] = z

        def values(c):
            nc.vector.quantize_mx(out=z_word[c][:].bitcast(FP8X4), scales=z_scale[c][:], in_=z_tile[c][:].rearrange("p j t -> p (j t)"))
            per_bank = PACK // len(SUM_BANKS[c])
            acc = [psum.tile([P, per_bank, CHUNK], F32, name="sum%d_%d" % (c, e), tag=bank) for e, bank in enumerate(SUM_BANKS[c])]
            for t in range(PACK):
                nc.tensor.matmul_mx(
                    out=acc[t // per_bank][:, t % per_bank, :],
                    lhsT=w_word[:, 2 * t * P : 2 * (t + 1) * P].bitcast(FP4X4),
                    lhsT_scale=w_scale[:, t * P : (t + 1) * P],
                    rhs=z_word[c][:].bitcast(FP8X4),
                    rhs_scale=z_scale[c][:],
                    start=True,
                    stop=True,
                )
            sum_bank[c] = acc

        def result(c):
            y = keep.tile([P, PACK, CHUNK], F32, name="y%d" % c, align_bytes=DMA_ALIGN)
            per_bank = PACK // len(sum_bank[c])
            for e, acc in enumerate(sum_bank[c]):
                nc.vector.tensor_tensor(y[:, e * per_bank : (e + 1) * per_bank, :], acc[:], factor[:, queries(c)].unsqueeze(1).broadcast_to([P, per_bank, CHUNK]), MULT)
            nc.sync.dma_start(out_rows[:, :, queries(c)], y[:])
            y_tile[c] = y

        def weave(c, copy):
            woven = keep.tile([P, CHUNK, PACK], BF16, name="y_woven%d" % c, tag="relu" if c == 0 else "y_woven%d" % c, align_bytes=64)
            copy(woven_side(woven[:]), slot_side(y_tile[c][:]))
            y_woven[c] = woven

        def weave_shared(c):
            woven = keep.tile([P, CHUNK, PACK], BF16, name="y_woven%d" % c, align_bytes=64)
            for copy, part in ((nc.scalar.copy, slice(0, SCALAR_COLUMNS)), (nc.vector.tensor_copy, slice(SCALAR_COLUMNS, CHUNK))):
                copy(woven_side(woven[:, part, :]), slot_side(y_tile[c][:, :, part]))
            y_woven[c] = woven

        def result_planes(c):
            nc.vector.quantize_mx(out=y_word[:, queries(c)].bitcast(FP8X4), scales=y_scale[:, queries(c)], in_=y_woven[c][:].rearrange("p j t -> p (j t)"))
            if c % 2 == 1:
                first = (c - 1) * CHUNK
                nc.sync.dma_start(out_words[:, PACK * first : PACK * (first + HALF)].bitcast(I32), y_word[:, first : first + HALF].bitcast(I32))

        for c in range(CHUNKS):
            if c < len(QUERY_PIECES):
                gather_queries(c)
            scores(c)
        nc.sync.dma_start(factor[:], cnt)
        nc.scalar.copy(slots_of(w_word[:].bitcast(U16), LINE // 2), columns_of(w_word_raw[:].bitcast(U16), LINE // 2))

        for c in range(LAST):
            weigh(c)
        square(LAST)

        z_from_scores(0, 0)
        z_from_scores(0, 1)
        z_from_scores(1, 0)
        values(0)
        z_from_scores(1, 1)
        z_from_scores(2, 0)
        values(1)
        result(0)
        values(2)
        z_from_size(LAST)
        result(1)
        values(LAST)
        result(2)
        for c in range(LAST):
            weave(c, nc.scalar.copy)
        result(LAST)
        result_planes(0)
        result_planes(1)
        weave_shared(LAST)
        result_planes(2)
        result_planes(LAST)

        for q in range(P // QUADRANT):
            queue = nc.scalar if q % 2 == 0 else nc.sync
            queue.dma_start(out_2[0][PACK * q : PACK * (q + 1), :].bitcast(I32), y_scale[QUADRANT * q : QUADRANT * q + PACK, :].bitcast(I32))
